import numpy as np
import ml_dtypes


def mxq(x, axis, fmt="e4m3"):
    dtype, down = {"e4m3": (ml_dtypes.float8_e4m3fn, 7), "e5m2": (ml_dtypes.float8_e5m2, 14)}[fmt]
    v = np.moveaxis(np.asarray(x, np.float32).astype(ml_dtypes.bfloat16).astype(np.float64), axis, -1)
    blocks = v.reshape(v.shape[:-1] + (-1, 32))
    amax = np.abs(blocks).max(-1, keepdims=True)
    byte = np.maximum(np.where(amax > 0, np.frexp(amax)[1] - 1 + 127, 0) - down, 1)
    scale = np.exp2(byte - 127.0)
    codes = (blocks / scale).astype(np.float32).astype(dtype).astype(np.float64)
    return np.moveaxis((codes * scale).reshape(v.shape), -1, axis)


WIDE = False


def mx_kscale(k):
    if not WIDE:
        return np.ones(k)
    levels = np.array([10, -10, 5, -5, 0])
    if k % 512:
        return np.exp2(np.random.permutation(np.resize(levels, k // 32))).repeat(32)
    a = np.empty((k // 512, 16))
    for p in range(k // 512):
        a[p, :8] = np.random.permutation(np.resize(levels, 8))
        for g in range(8):
            far = levels[np.abs(levels - a[p, g]) >= 10]
            a[p, g + 8] = far[np.random.randint(len(far))]
    return np.exp2(a.ravel()).repeat(32)


def f64(x):
    return np.asarray(x).astype(np.float64)


def striped(idx):
    return np.tile(idx.reshape(-1, 16).T, (8, 1)).astype(np.uint16)


def unstriped(offs):
    return offs[:16].T.reshape(-1).astype(np.int64)


E2M1 = np.array([0.0, 0.5, 1.0, 1.5, 2.0, 3.0, 4.0, 6.0, -0.0, -0.5, -1.0, -1.5, -2.0, -3.0, -4.0, -6.0])


def pack_weight(w, fmt):
    k, n = w.shape
    w = f64(np.asarray(w, np.float32).astype(ml_dtypes.bfloat16)).reshape(k // 32, 32, n)
    amax = np.abs(w).max(1)
    if fmt == "e4m3":
        byte = np.frexp(amax)[1] - 1 + 127 - 7
    else:
        mant, ex = np.frexp(amax / 6.0)
        byte = np.where(mant > 0.5, ex, ex - 1) + 127
    byte = np.clip(np.where(amax > 0, byte, 1), 1, 254)
    scaled = (w * np.exp2(127.0 - byte)[:, None, :]).reshape(k, n).astype(np.float32)
    by_word = np.ascontiguousarray(scaled.reshape(k // 512, 128, 4, n).transpose(0, 1, 3, 2))
    if fmt == "e4m3":
        words = by_word.astype(ml_dtypes.float8_e4m3fn).view(np.uint8)
    else:
        c = by_word.astype(ml_dtypes.float4_e2m1fn).view(np.uint8) & 0xF
        words = (c[..., 0::2] | (c[..., 1::2] << 4)).reshape(k // 512, 128, 2 * n)
    return np.ascontiguousarray(words), np.ascontiguousarray(byte.astype(np.uint8).reshape(k // 512, 16, n))


def unpack_weight(words, scales, fmt):
    g, _, n = scales.shape
    words = np.ascontiguousarray(words).reshape(g, 128, n, -1)
    if fmt == "e4m3":
        vals = words.view(ml_dtypes.float8_e4m3fn).astype(np.float64)
    else:
        nib = np.empty((g, 128, n, 4), np.uint8)
        nib[..., 0::2] = words & 0xF
        nib[..., 1::2] = words >> 4
        vals = E2M1[nib]
    vals = vals * np.repeat(np.exp2(scales.astype(np.float64) - 127.0), 8, axis=1)[..., None]
    return vals.transpose(0, 1, 3, 2).reshape(g * 512, n)


def planes(y):
    n, m = y.shape
    v = y.astype(np.float32).astype(ml_dtypes.bfloat16).astype(np.float64).reshape(n // 32, 32, m)
    top = np.abs(v).max(1)
    byte = np.clip(np.where(top > 0, np.frexp(top)[1] - 1 + 127 - 7, 1), 1, 254)
    codes = (v * np.exp2(127.0 - byte)[:, None, :]).reshape(n, m).astype(np.float32).astype(ml_dtypes.float8_e4m3fn).view(np.uint8)
    words = codes.reshape(n // 512, 128, 4, m).transpose(0, 1, 3, 2)
    return np.ascontiguousarray(words), np.ascontiguousarray(byte.astype(np.uint8).reshape(n // 512, 16, m))


K, T, E, C, H, N = 1024, 512, 4, 128, 512, 512


def by_expert(wq, xq):
    return np.concatenate([wq[e].T @ xq[:, e * C:(e + 1) * C] for e in range(E)], axis=1)


def setup_inputs():
    n = np.random.standard_normal
    s = mx_kscale(K)
    u = mx_kscale(H)
    slot_token = np.concatenate([np.random.permutation(T)[:C] for e in range(E)])
    partner = np.concatenate([np.random.permutation(T) for _ in range(-(-E * C // T))])[:E * C]
    x = pack_weight(n((K, T)) * s[:, None], "e4m3")
    wp = [pack_weight(m, "e2m1") for m in n((E, K, H)) / np.sqrt(K) / s[None, :, None] * u]
    return {
        "x_words": x[0],
        "x_scales": x[1],
        "w1": (n((E, K, H)) / np.sqrt(K) / s[None, :, None] * u).astype(np.float32),
        "wp_words": np.stack([m[0] for m in wp]),
        "wp_scales": np.stack([m[1] for m in wp]),
        "w2": (n((E, H, N)) / np.sqrt(H) / u[None, :, None]).astype(np.float32),
        "offs": striped(slot_token),
        "offs2": striped(partner),
    }


def reference(x_words, x_scales, w1, wp_words, wp_scales, w2, offs, offs2):
    w1q = mxq(f64(w1), 1, "e4m3")
    wp = np.stack([unpack_weight(wp_words[e], wp_scales[e], "e2m1") for e in range(E)])
    w2q = mxq(f64(w2), 1, "e4m3")
    idx, idx2 = unstriped(offs), unstriped(offs2)
    x = unpack_weight(x_words, x_scales, "e4m3")
    h = by_expert(w1q, x[:, idx]) + by_expert(wp, x[:, idx2])
    y = by_expert(w2q, mxq(h, 0, "e4m3"))
    out = y
    out_0 = out
    return (out_0,) + planes(out_0)

@@ -1,0 +1,253 @@
+from contextlib import ExitStack
+
+import concourse.mybir as mybir
+from concourse.masks import make_identity
+
+F32 = mybir.dt.float32
+BF16 = mybir.dt.bfloat16
+I32 = mybir.dt.int32
+U32 = mybir.dt.uint32
+U16 = mybir.dt.uint16
+U8 = mybir.dt.uint8
+FP8X4 = mybir.dt.float8_e4m3fn_x4
+FP4X4 = mybir.dt.float4_e2m1fn_x4
+
+K, T, E, C, H, N = 1024, 512, 4, 128, 512, 512
+P = 128
+PACK = 4
+PASSES = K // (P * PACK)
+SLOTS = E * C
+HALF = 256
+WINDOW = 768
+FLOPS = 2 * SLOTS * (2 * K * H + H * N)
+SCALAR_SHARE = 20
+
+
+def tile_moe_duo_s_none_kernel(
+    tc, x_words, x_scales, w1, wp_words, wp_scales, w2, offs, offs2, out_0, out_1, out_2
+):
+    nc = tc.nc
+    last = E - 1
+    with ExitStack() as ctx:
+        keep = ctx.enter_context(tc.tile_pool(name="keep", bufs=1))
+        ring = ctx.enter_context(tc.tile_pool(name="ring", bufs=3))
+        psum = ctx.enter_context(tc.psum_pool(name="psum", bufs=2))
+
+        lists = [keep.tile([P, SLOTS // 16], U16, name="list%d" % a) for a in range(2)]
+        xw = keep.tile([P, T + WINDOW], U32, name="xw", align_bytes=64)
+        xs = keep.tile([P, T + WINDOW], U8, name="xs", align_bytes=64)
+        wps = keep.tile([P, E * PASSES * H], U8, name="wps", align_bytes=64)
+        wp = [keep.tile([P, PASSES, 2 * H], U8, name="wp%d" % e, align_bytes=64) for e in range(E)]
+        w1_raw = [[keep.tile([P, PACK, H], F32, name="w1r%d_%d" % (e, s), align_bytes=64) for s in range(PASSES)] for e in range(E)]
+        w2_raw = [keep.tile([P, PACK, N], F32, name="w2r%d" % e, align_bytes=64) for e in range(last)]
+        w2_tail = [keep.tile([P, PACK, HALF], F32, name="w2t%d" % h) for h in range(2)]
+        ident = keep.tile([P, P], F32, name="ident")
+
+        nc.gpsimd.memset(xs[:].bitcast(I32), 0)
+        nc.vector.memset(xw[:, PASSES * T :].bitcast(I32), 0)
+        nc.vector.memset(wps[:].bitcast(I32), 0)
+        make_identity(nc, ident[:])
+
+        def load_w1(e, s):
+            rows = w1[e, s * 512 : (s + 1) * 512, :]
+            nc.sync.dma_start(out=w1_raw[e][s][:], in_=rows.rearrange("(p j) c -> p j c", j=PACK))
+
+        def load_wp(e):
+            nc.sync.dma_start(out=wp[e][:].bitcast(I32), in_=wp_words[e].bitcast(I32).rearrange("s p c -> p s c"))
+
+        def load_w2(e):
+            src = w2[e].rearrange("(p j) c -> p j c", j=PACK)
+            if e < last:
+                nc.sync.dma_start(out=w2_raw[e][:], in_=src)
+            else:
+                for h in range(2):
+                    nc.sync.dma_start(out=w2_tail[h][:], in_=src[:, :, h * HALF : (h + 1) * HALF])
+
+        nc.sync.dma_start(
+            out=xw[:, 0 : PASSES * T].bitcast(I32).rearrange("p (s t) -> p s t", s=PASSES),
+            in_=x_words.rearrange("s p t d -> p s (t d)").bitcast(I32),
+        )
+        nc.sync.dma_start(out=lists[0][:], in_=offs)
+        nc.sync.dma_start(out=lists[1][:], in_=offs2)
+        xs_src = x_scales.bitcast(I32).rearrange("s (q r) c -> r q s c", r=4)
+        xs_dst = xs[:, 0 : PASSES * T].bitcast(I32).rearrange("p (s c) -> p s c", s=PASSES)
+        for r in range(4):
+            nc.sync.dma_start(out=xs_dst[r:P:32], in_=xs_src[r])
+        load_wp(0)
+        for e in range(E):
+            load_w1(e, 0)
+            if e == 1:
+                wps_src = wp_scales.bitcast(I32).rearrange("e s (q r) c -> r q (e s) c", r=4)
+                wps_dst = wps[:].bitcast(I32).rearrange("p (g c) -> p g c", g=E * PASSES)
+                for r in range(4):
+                    nc.sync.dma_start(out=wps_dst[r:P:32], in_=wps_src[r])
+            if e >= 2:
+                load_w2(e - 2)
+            load_w1(e, 1)
+            if e < last:
+                load_wp(e + 1)
+        load_w2(last - 1)
+        load_w2(last)
+
+        gw = [[keep.tile([P, SLOTS], U32, name="gw%d_%d" % (a, s), align_bytes=64) for s in range(PASSES)] for a in range(2)]
+        gs = [[keep.tile([P, SLOTS], U8, name="gs%d_%d" % (a, s), align_bytes=64) for s in range(PASSES)] for a in range(2)]
+        for a in (1, 0):
+            for s in range(PASSES):
+                nc.vector.tensor_copy(gw[a][s][:], xw[:, s * T : s * T + WINDOW].indirect(lists[a][:]))
+                nc.vector.tensor_copy(gs[a][s][:], xs[:, s * T : s * T + WINDOW].indirect(lists[a][:]))
+
+        y_codes = keep.tile([P, SLOTS], U32, name="y_codes", align_bytes=64)
+        y_scales = keep.tile([P, SLOTS], U8, name="y_scales", align_bytes=64)
+        out0 = out_0.rearrange("(p t) j -> p t j", t=PACK)
+        out1 = out_1[0].rearrange("p j d -> p (j d)").bitcast(I32)
+
+        h_banks, turned, h_quant, w2_quant, y_staged = {}, {}, {}, {}, {}
+
+        def copy_on(on_scalar, out, in_):
+            if on_scalar:
+                nc.scalar.copy(out=out, in_=in_)
+            else:
+                nc.vector.tensor_copy(out=out, in_=in_)
+
+        def partner_passes(e):
+            slots = slice(e * C, (e + 1) * C)
+            bank = psum.tile([P, H], F32, name="h_bank")
+            h_banks[e] = bank
+            for s in range(PASSES):
+                plane = (e * PASSES + s) * H
+                nc.tensor.matmul_mx(
+                    out=bank[:], lhsT=gw[1][s][:, slots].bitcast(FP8X4), lhsT_scale=gs[1][s][:, slots],
+                    rhs=wp[e][:, s, :].bitcast(FP4X4), rhs_scale=wps[:, plane : plane + H], start=(s == 0), stop=False,
+                )
+
+        def w1_pass(e, s):
+            slots = slice(e * C, (e + 1) * C)
+            grouped = ring.tile([P, H * PACK], BF16, name="grouped", bufs=4, align_bytes=64)
+            for h in range(2):
+                copy_on(
+                    h == 0 or e == 0,
+                    grouped[:, h * HALF * PACK : (h + 1) * HALF * PACK].rearrange("p (c i j) -> p c j i", i=4, j=PACK),
+                    w1_raw[e][s][:, :, h * HALF : (h + 1) * HALF].rearrange("p j (c i) -> p c j i", i=4),
+                )
+            codes = ring.tile([P, H], U32, name="w1c", align_bytes=64)
+            scales = ring.tile([P, H], U8, name="w1s", align_bytes=64)
+            nc.vector.quantize_mx(out=codes[:].bitcast(FP8X4), scales=scales[:], in_=grouped[:])
+            nc.tensor.matmul_mx(
+                out=h_banks[e][:], lhsT=gw[0][s][:, slots].bitcast(FP8X4), lhsT_scale=gs[0][s][:, slots],
+                rhs=codes[:].bitcast(FP8X4), rhs_scale=scales[:], start=False, stop=(s == PASSES - 1),
+            )
+
+        def spent(raw):
+            return raw[:, 0, 0:HALF].bitcast(BF16)
+
+        def turn_h(e, pairs):
+            nc.scalar.copy(
+                out=pairs.rearrange("s (u p d) -> s u p d", u=2, d=2),
+                in_=h_banks[e][:].rearrange("s (p u d) -> s u p d", u=2, d=2),
+            )
+            bank = psum.tile([P, 2, C], F32, name="turned")
+            turned[e] = bank
+            for u in range(2):
+                nc.tensor.transpose(bank[:, u, :], pairs.bitcast(F32)[:, u * P : (u + 1) * P], ident[:])
+
+        def quantise_h(e, grouped):
+            nc.scalar.copy(
+                out=grouped.bitcast(F32).rearrange("p (s u) -> p s u", u=2),
+                in_=turned[e][:].rearrange("p u s -> p s u"),
+            )
+            codes = ring.tile([P, C], U32, name="hc", align_bytes=64)
+            scales = ring.tile([P, C], U8, name="hs", align_bytes=64)
+            nc.vector.quantize_mx(out=codes[:].bitcast(FP8X4), scales=scales[:], in_=grouped)
+            h_quant[e] = (codes, scales)
+
+        def open_w2(e):
+            grouped = ring.tile([P, PACK, P * PACK], BF16, name="grouped", bufs=4, align_bytes=64)
+            codes = ring.tile([P, N], U32, name="w2c", align_bytes=64)
+            scales = ring.tile([P, N], U8, name="w2s", align_bytes=64)
+            w2_quant[e] = (codes, scales)
+            return grouped
+
+        def w2_views(grouped, raw, h):
+            dst = grouped[:, :, h * HALF : (h + 1) * HALF].rearrange("p t (m j) -> p m j t", j=PACK)
+            return dst, raw.rearrange("p j (m t) -> p m j t", t=PACK)
+
+        def quantise_w2(e):
+            grouped = open_w2(e)
+            for h in range(2):
+                dst, src = w2_views(grouped, w2_raw[e][:, :, h * HALF : (h + 1) * HALF], h)
+                copy_on(h == 0, dst, src)
+            codes, scales = w2_quant[e]
+            nc.vector.quantize_mx(out=codes[:].bitcast(FP8X4), scales=scales[:], in_=grouped[:].rearrange("p t c -> p (t c)"))
+
+        def quantise_w2_half(grouped, h):
+            dst, src = w2_views(grouped, w2_tail[h][:], h)
+            share = SCALAR_SHARE if h == 0 else 0
+            if share:
+                nc.scalar.copy(out=dst[:, 0:share], in_=src[:, 0:share])
+            nc.vector.tensor_copy(out=dst[:, share:64], in_=src[:, share:64])
+            codes, scales = w2_quant[last]
+            for t in range(PACK):
+                words = slice(t * P + h * 64, t * P + (h + 1) * 64)
+                nc.vector.quantize_mx(
+                    out=codes[:, words].bitcast(FP8X4), scales=scales[:, words],
+                    in_=grouped[:, t, h * HALF : (h + 1) * HALF],
+                )
+
+        def second_layer(e, staged):
+            codes, scales = w2_quant[e]
+            hc, hs = h_quant[e]
+            bank = psum.tile([P, PACK, C], F32, name="y_bank")
+            for t in range(PACK):
+                words = slice(t * P, (t + 1) * P)
+                nc.tensor.matmul_mx(
+                    out=bank[:, t, :], lhsT=codes[:, words].bitcast(FP8X4), lhsT_scale=scales[:, words],
+                    rhs=hc[:].bitcast(FP8X4), rhs_scale=hs[:], start=True, stop=True,
+                )
+            slots = slice(e * C, (e + 1) * C)
+            grouped = ring.tile([P, C * PACK], BF16, name="y_grouped", align_bytes=64)
+            interleaved = grouped[:].rearrange("p (s t) -> p s t", t=PACK)
+            if e < last:
+                nc.scalar.copy(out=staged, in_=bank[:])
+                nc.vector.tensor_copy(out=interleaved, in_=staged.rearrange("p t s -> p s t"))
+            else:
+                nc.vector.tensor_copy(out=interleaved, in_=bank[:].rearrange("p t s -> p s t"))
+                nc.scalar.copy(out=staged, in_=bank[:])
+            nc.vector.quantize_mx(out=y_codes[:, slots].bitcast(FP8X4), scales=y_scales[:, slots], in_=grouped[:])
+            y_staged[e] = staged
+
+        partner_passes(0)
+        for e in range(E):
+            w1_pass(e, 0)
+            if e >= 1:
+                turn_h(e - 1, spent(w1_raw[e][0]))
+            if e >= 2:
+                quantise_w2(e - 2)
+                quantise_h(e - 1, spent(w2_raw[e - 2]))
+            w1_pass(e, 1)
+            if e == 1:
+                quantise_h(0, spent(w1_raw[1][1]))
+            if e >= 2:
+                second_layer(e - 2, w1_raw[e][1][:, :, 0:C])
+            if e < last:
+                partner_passes(e + 1)
+        quantise_w2(last - 1)
+        turn_h(last, spent(w2_raw[last - 1]))
+        tail_grouped = open_w2(last)
+        quantise_w2_half(tail_grouped, 0)
+        h_tail = keep.tile([P, C * PACK], BF16, name="h_tail", align_bytes=64)
+        quantise_h(last, h_tail[:])
+        y_tail = [keep.tile([P, PACK, C], F32, name="y_tail%d" % i) for i in range(2)]
+        second_layer(last - 1, y_tail[0][:])
+        quantise_w2_half(tail_grouped, 1)
+        second_layer(last, y_tail[1][:])
+
+        for e in range(last):
+            nc.sync.dma_start(out=out0[:, :, e * C : (e + 1) * C], in_=y_staged[e])
+        nc.sync.dma_start(out=out1[:, 0 : last * C], in_=y_codes[:, 0 : last * C].bitcast(I32))
+        nc.scalar.dma_start(out=out0[:, :, last * C : SLOTS], in_=y_staged[last])
+        nc.sync.dma_start(out=out1[:, last * C : SLOTS], in_=y_codes[:, last * C : SLOTS].bitcast(I32))
+        for q in range(4):
+            nc.sync.dma_start(
+                out=out_2[0, 4 * q : 4 * q + 4, :].bitcast(I32),
+                in_=y_scales[32 * q : 32 * q + 4, :].bitcast(I32),
+            )

@@ -35,17 +35,20 @@ def tile_moe_duo_s_none_kernel(
 
         lists = [keep.tile([P, SLOTS // 16], U16, name="list%d" % a) for a in range(2)]
         xw = keep.tile([P, T + WINDOW], U32, name="xw", align_bytes=64)
-        xs = keep.tile([P, T + WINDOW], U8, name="xs", align_bytes=64)
+        xs = keep.tile([P, WINDOW], U8, name="xs", align_bytes=64)
         wps = keep.tile([P, E * PASSES * H], U8, name="wps", align_bytes=64)
         wp = [keep.tile([P, PASSES, 2 * H], U8, name="wp%d" % e, align_bytes=64) for e in range(E)]
         w1_raw = [[keep.tile([P, PACK, H], F32, name="w1r%d_%d" % (e, s), align_bytes=64) for s in range(PASSES)] for e in range(E)]
         w2_raw = [keep.tile([P, PACK, N], F32, name="w2r%d" % e, align_bytes=64) for e in range(last)]
         w2_tail = [keep.tile([P, PACK, HALF], F32, name="w2t%d" % h) for h in range(2)]
+        xs_rows = keep.tile([P, T // 4], I32, name="xs_rows")
+        moved = keep.tile([P, SLOTS], U8, name="moved", align_bytes=64)
         ident = keep.tile([P, P], F32, name="ident")
 
         nc.gpsimd.memset(xs[:].bitcast(I32), 0)
         nc.vector.memset(xw[:, PASSES * T :].bitcast(I32), 0)
         nc.vector.memset(wps[:].bitcast(I32), 0)
+        nc.gpsimd.memset(moved[:].bitcast(I32), 0)
         make_identity(nc, ident[:])
 
         def load_w1(e, s):
@@ -69,32 +72,45 @@ def tile_moe_duo_s_none_kernel(
         )
         nc.sync.dma_start(out=lists[0][:], in_=offs)
         nc.sync.dma_start(out=lists[1][:], in_=offs2)
-        xs_src = x_scales.bitcast(I32).rearrange("s (q r) c -> r q s c", r=4)
-        xs_dst = xs[:, 0 : PASSES * T].bitcast(I32).rearrange("p (s c) -> p s c", s=PASSES)
-        for r in range(4):
-            nc.sync.dma_start(out=xs_dst[r:P:32], in_=xs_src[r])
+        load_w1(0, 0)
+        for q in range(4):
+            nc.sync.dma_start(
+                out=xs_rows[32 * q : 32 * q + 4 * PASSES, :],
+                in_=x_scales[:, 4 * q : 4 * q + 4, :].bitcast(I32),
+            )
+        load_w1(0, 1)
         load_wp(0)
-        for e in range(E):
-            load_w1(e, 0)
-            if e == 1:
-                wps_src = wp_scales.bitcast(I32).rearrange("e s (q r) c -> r q (e s) c", r=4)
-                wps_dst = wps[:].bitcast(I32).rearrange("p (g c) -> p g c", g=E * PASSES)
-                for r in range(4):
-                    nc.sync.dma_start(out=wps_dst[r:P:32], in_=wps_src[r])
-            if e >= 2:
-                load_w2(e - 2)
-            load_w1(e, 1)
-            if e < last:
-                load_wp(e + 1)
-        load_w2(last - 1)
-        load_w2(last)
+        load_wp(1)
+        load_w1(1, 0)
+        wps_src = wp_scales.bitcast(I32).rearrange("e s (q r) c -> r q (e s) c", r=4)
+        wps_dst = wps[:].bitcast(I32).rearrange("p (g c) -> p g c", g=E * PASSES)
+        for r in range(4):
+            nc.sync.dma_start(out=wps_dst[r:P:32], in_=wps_src[r])
+        load_w1(1, 1)
 
         gw = [[keep.tile([P, SLOTS], U32, name="gw%d_%d" % (a, s), align_bytes=64) for s in range(PASSES)] for a in range(2)]
-        gs = [[keep.tile([P, SLOTS], U8, name="gs%d_%d" % (a, s), align_bytes=64) for s in range(PASSES)] for a in range(2)]
+        gs = [keep.tile([P, SLOTS], U8, name="gs%d" % a, align_bytes=64) for a in range(2)]
+        for q in range(4):
+            rows = slice(32 * q, 32 * q + 4 * PASSES)
+            nc.vector.tensor_copy(out=xs[:, 0:T].bitcast(I32)[rows, :], in_=xs_rows[rows, :])
+        for a in (1, 0):
+            nc.vector.tensor_copy(gs[a][:], xs[:].indirect(lists[a][:]))
         for a in (1, 0):
             for s in range(PASSES):
                 nc.vector.tensor_copy(gw[a][s][:], xw[:, s * T : s * T + WINDOW].indirect(lists[a][:]))
-                nc.vector.tensor_copy(gs[a][s][:], xs[:, s * T : s * T + WINDOW].indirect(lists[a][:]))
+        for q in range(4):
+            nc.sync.dma_start(
+                out=moved[32 * q : 32 * q + 4, :].bitcast(I32),
+                in_=gs[1][32 * q + 4 : 32 * q + 8, :].bitcast(I32),
+            )
+        for e in range(2, E):
+            load_wp(e)
+            load_w1(e, 0)
+            load_w2(e - 2)
+            load_w1(e, 1)
+        load_w2(last - 1)
+        load_w2(last)
+        partner_scales = (gs[1], moved)
 
         y_codes = keep.tile([P, SLOTS], U32, name="y_codes", align_bytes=64)
         y_scales = keep.tile([P, SLOTS], U8, name="y_scales", align_bytes=64)
@@ -109,16 +125,15 @@ def tile_moe_duo_s_none_kernel(
             else:
                 nc.vector.tensor_copy(out=out, in_=in_)
 
-        def partner_passes(e):
+        def partner_pass(e, s, stop=False):
             slots = slice(e * C, (e + 1) * C)
-            bank = psum.tile([P, H], F32, name="h_bank")
-            h_banks[e] = bank
-            for s in range(PASSES):
-                plane = (e * PASSES + s) * H
-                nc.tensor.matmul_mx(
-                    out=bank[:], lhsT=gw[1][s][:, slots].bitcast(FP8X4), lhsT_scale=gs[1][s][:, slots],
-                    rhs=wp[e][:, s, :].bitcast(FP4X4), rhs_scale=wps[:, plane : plane + H], start=(s == 0), stop=False,
-                )
+            if s == 0:
+                h_banks[e] = psum.tile([P, H], F32, name="h_bank")
+            plane = (e * PASSES + s) * H
+            nc.tensor.matmul_mx(
+                out=h_banks[e][:], lhsT=gw[1][s][:, slots].bitcast(FP8X4), lhsT_scale=partner_scales[s][:, slots],
+                rhs=wp[e][:, s, :].bitcast(FP4X4), rhs_scale=wps[:, plane : plane + H], start=(s == 0), stop=stop,
+            )
 
         def w1_pass(e, s):
             slots = slice(e * C, (e + 1) * C)
@@ -133,8 +148,8 @@ def tile_moe_duo_s_none_kernel(
             scales = ring.tile([P, H], U8, name="w1s", align_bytes=64)
             nc.vector.quantize_mx(out=codes[:].bitcast(FP8X4), scales=scales[:], in_=grouped[:])
             nc.tensor.matmul_mx(
-                out=h_banks[e][:], lhsT=gw[0][s][:, slots].bitcast(FP8X4), lhsT_scale=gs[0][s][:, slots],
-                rhs=codes[:].bitcast(FP8X4), rhs_scale=scales[:], start=False, stop=(s == PASSES - 1),
+                out=h_banks[e][:], lhsT=gw[0][s][:, slots].bitcast(FP8X4), lhsT_scale=gs[0][4 * s : P, slots],
+                rhs=codes[:].bitcast(FP8X4), rhs_scale=scales[:], start=False, stop=(s == PASSES - 1 and e > 0),
             )
 
         def spent(raw):
@@ -196,26 +211,25 @@ def tile_moe_duo_s_none_kernel(
         def second_layer(e, staged):
             codes, scales = w2_quant[e]
             hc, hs = h_quant[e]
-            bank = psum.tile([P, PACK, C], F32, name="y_bank")
+            banks = [psum.tile([P, PACK, C], F32, name="y_bank", bufs=3) for i in range(2 if e == last else 1)]
             for t in range(PACK):
                 words = slice(t * P, (t + 1) * P)
                 nc.tensor.matmul_mx(
-                    out=bank[:, t, :], lhsT=codes[:, words].bitcast(FP8X4), lhsT_scale=scales[:, words],
+                    out=banks[t * len(banks) // PACK][:, t, :], lhsT=codes[:, words].bitcast(FP8X4), lhsT_scale=scales[:, words],
                     rhs=hc[:].bitcast(FP8X4), rhs_scale=hs[:], start=True, stop=True,
                 )
             slots = slice(e * C, (e + 1) * C)
             grouped = ring.tile([P, C * PACK], BF16, name="y_grouped", align_bytes=64)
-            interleaved = grouped[:].rearrange("p (s t) -> p s t", t=PACK)
             if e < last:
-                nc.scalar.copy(out=staged, in_=bank[:])
-                nc.vector.tensor_copy(out=interleaved, in_=staged.rearrange("p t s -> p s t"))
+                nc.scalar.copy(out=staged, in_=banks[0][:])
             else:
-                nc.vector.tensor_copy(out=interleaved, in_=bank[:].rearrange("p t s -> p s t"))
-                nc.scalar.copy(out=staged, in_=bank[:])
+                nc.scalar.copy(out=staged[:, 0:2, :], in_=banks[0][:, 0:2, :])
+                nc.vector.tensor_copy(out=staged[:, 2:4, :], in_=banks[1][:, 2:4, :])
+            nc.vector.tensor_copy(out=grouped[:].rearrange("p (s t) -> p s t", t=PACK), in_=staged.rearrange("p t s -> p s t"))
             nc.vector.quantize_mx(out=y_codes[:, slots].bitcast(FP8X4), scales=y_scales[:, slots], in_=grouped[:])
             y_staged[e] = staged
 
-        partner_passes(0)
+        partner_pass(0, 0)
         for e in range(E):
             w1_pass(e, 0)
             if e >= 1:
@@ -224,12 +238,15 @@ def tile_moe_duo_s_none_kernel(
                 quantise_w2(e - 2)
                 quantise_h(e - 1, spent(w2_raw[e - 2]))
             w1_pass(e, 1)
+            if e == 0:
+                partner_pass(0, 1, stop=True)
             if e == 1:
                 quantise_h(0, spent(w1_raw[1][1]))
             if e >= 2:
                 second_layer(e - 2, w1_raw[e][1][:, :, 0:C])
             if e < last:
-                partner_passes(e + 1)
+                partner_pass(e + 1, 0)
+                partner_pass(e + 1, 1)
         quantise_w2(last - 1)
         turn_h(last, spent(w2_raw[last - 1]))
         tail_grouped = open_w2(last)

@@ -20,7 +20,13 @@ SLOTS = E * C
 HALF = 256
 WINDOW = 768
 FLOPS = 2 * SLOTS * (2 * K * H + H * N)
-SCALAR_SHARE = 20
+MERGED = ()
+SHARE_LAST = 48
+SHARE_F = 36
+SHARE_W1 = 64
+SHARE_W2 = 64
+SHARE_A = 36
+SHARE_B = 0
 
 
 def tile_moe_duo_s_none_kernel(
@@ -37,10 +43,18 @@ def tile_moe_duo_s_none_kernel(
         xw = keep.tile([P, T + WINDOW], U32, name="xw", align_bytes=64)
         xs = keep.tile([P, WINDOW], U8, name="xs", align_bytes=64)
         wps = keep.tile([P, E * PASSES * H], U8, name="wps", align_bytes=64)
-        wp = [keep.tile([P, PASSES, 2 * H], U8, name="wp%d" % e, align_bytes=64) for e in range(E)]
-        w1_raw = [[keep.tile([P, PACK, H], F32, name="w1r%d_%d" % (e, s), align_bytes=64) for s in range(PASSES)] for e in range(E)]
+        wp_all = keep.tile([P, E * PASSES, 2 * H], U8, name="wp_all", align_bytes=64)
+        wp = [wp_all[:, g, :] for g in range(E * PASSES)]
+        w1_both = {e: keep.tile([P, PASSES, PACK, H], F32, name="w1r%d" % e, align_bytes=64) for e in MERGED}
+        w1_one = {
+            (e, s): keep.tile([P, PACK, H], F32, name="w1r%d_%d" % (e, s), align_bytes=64)
+            for e in range(E) for s in range(PASSES) if e not in MERGED
+        }
+        w1_raw = {(e, s): w1_both[e][:, s] for e in MERGED for s in range(PASSES)}
+        for key in w1_one:
+            w1_raw[key] = w1_one[key][:]
         w2_raw = [keep.tile([P, PACK, N], F32, name="w2r%d" % e, align_bytes=64) for e in range(last)]
-        w2_tail = [keep.tile([P, PACK, HALF], F32, name="w2t%d" % h) for h in range(2)]
+        w2_tail = [keep.tile([P, PACK, HALF], F32, name="w2t%d" % h, align_bytes=64) for h in range(2)]
         xs_rows = keep.tile([P, T // 4], I32, name="xs_rows")
         moved = keep.tile([P, SLOTS], U8, name="moved", align_bytes=64)
         ident = keep.tile([P, P], F32, name="ident")
@@ -51,12 +65,13 @@ def tile_moe_duo_s_none_kernel(
         nc.gpsimd.memset(moved[:].bitcast(I32), 0)
         make_identity(nc, ident[:])
 
-        def load_w1(e, s):
-            rows = w1[e, s * 512 : (s + 1) * 512, :]
-            nc.sync.dma_start(out=w1_raw[e][s][:], in_=rows.rearrange("(p j) c -> p j c", j=PACK))
-
-        def load_wp(e):
-            nc.sync.dma_start(out=wp[e][:].bitcast(I32), in_=wp_words[e].bitcast(I32).rearrange("s p c -> p s c"))
+        def load_w1(e, passes=range(PASSES)):
+            src = w1[e].rearrange("(s p j) c -> p s (j c)", s=PASSES, j=PACK)
+            if e in MERGED:
+                nc.sync.dma_start(out=w1_both[e][:].rearrange("p s j c -> p s (j c)"), in_=src)
+            else:
+                for s in passes:
+                    nc.sync.dma_start(out=w1_one[e, s][:].rearrange("p j c -> p (j c)"), in_=src[:, s])
 
         def load_w2(e):
             src = w2[e].rearrange("(p j) c -> p j c", j=PACK)
@@ -70,80 +85,79 @@ def tile_moe_duo_s_none_kernel(
             out=xw[:, 0 : PASSES * T].bitcast(I32).rearrange("p (s t) -> p s t", s=PASSES),
             in_=x_words.rearrange("s p t d -> p s (t d)").bitcast(I32),
         )
-        nc.sync.dma_start(out=lists[0][:], in_=offs)
         nc.sync.dma_start(out=lists[1][:], in_=offs2)
-        load_w1(0, 0)
+        nc.sync.dma_start(out=lists[0][:], in_=offs)
         for q in range(4):
             nc.sync.dma_start(
                 out=xs_rows[32 * q : 32 * q + 4 * PASSES, :],
                 in_=x_scales[:, 4 * q : 4 * q + 4, :].bitcast(I32),
             )
-        load_w1(0, 1)
-        load_wp(0)
-        load_wp(1)
-        load_w1(1, 0)
+        load_w1(0)
         wps_src = wp_scales.bitcast(I32).rearrange("e s (q r) c -> r q (e s) c", r=4)
         wps_dst = wps[:].bitcast(I32).rearrange("p (g c) -> p g c", g=E * PASSES)
         for r in range(4):
             nc.sync.dma_start(out=wps_dst[r:P:32], in_=wps_src[r])
-        load_w1(1, 1)
+        load_w1(1, (0,))
+        nc.sync.dma_start(out=wp_all[:].bitcast(I32), in_=wp_words.bitcast(I32).rearrange("e s p c -> p (e s) c"))
+        load_w1(1, (1,))
 
         gw = [[keep.tile([P, SLOTS], U32, name="gw%d_%d" % (a, s), align_bytes=64) for s in range(PASSES)] for a in range(2)]
         gs = [keep.tile([P, SLOTS], U8, name="gs%d" % a, align_bytes=64) for a in range(2)]
+
+        def gather_words(a):
+            for s in range(PASSES):
+                nc.vector.tensor_copy(gw[a][s][:], xw[:, s * T : s * T + WINDOW].indirect(lists[a][:]))
+
+        gather_words(1)
         for q in range(4):
             rows = slice(32 * q, 32 * q + 4 * PASSES)
             nc.vector.tensor_copy(out=xs[:, 0:T].bitcast(I32)[rows, :], in_=xs_rows[rows, :])
-        for a in (1, 0):
-            nc.vector.tensor_copy(gs[a][:], xs[:].indirect(lists[a][:]))
-        for a in (1, 0):
-            for s in range(PASSES):
-                nc.vector.tensor_copy(gw[a][s][:], xw[:, s * T : s * T + WINDOW].indirect(lists[a][:]))
+        nc.vector.tensor_copy(gs[1][:], xs[:].indirect(lists[1][:]))
+        gather_words(0)
+        nc.vector.tensor_copy(gs[0][:], xs[:].indirect(lists[0][:]))
         for q in range(4):
             nc.sync.dma_start(
                 out=moved[32 * q : 32 * q + 4, :].bitcast(I32),
                 in_=gs[1][32 * q + 4 : 32 * q + 8, :].bitcast(I32),
             )
-        for e in range(2, E):
-            load_wp(e)
-            load_w1(e, 0)
-            load_w2(e - 2)
-            load_w1(e, 1)
-        load_w2(last - 1)
-        load_w2(last)
         partner_scales = (gs[1], moved)
+        load_w2(0)
+        load_w1(2, (0,))
+        load_w2(1)
+        load_w1(2, (1,))
+        load_w1(last)
+        load_w2(2)
+        load_w2(last)
 
         y_codes = keep.tile([P, SLOTS], U32, name="y_codes", align_bytes=64)
         y_scales = keep.tile([P, SLOTS], U8, name="y_scales", align_bytes=64)
         out0 = out_0.rearrange("(p t) j -> p t j", t=PACK)
         out1 = out_1[0].rearrange("p j d -> p (j d)").bitcast(I32)
 
-        h_banks, turned, h_quant, w2_quant, y_staged = {}, {}, {}, {}, {}
+        h_banks, turned, h_quant, w2_quant, y_banks, y_staged = {}, {}, {}, {}, {}, {}
 
-        def copy_on(on_scalar, out, in_):
-            if on_scalar:
-                nc.scalar.copy(out=out, in_=in_)
-            else:
-                nc.vector.tensor_copy(out=out, in_=in_)
-
-        def partner_pass(e, s, stop=False):
+        def partner_passes(e, passes=range(PASSES), stop=False):
             slots = slice(e * C, (e + 1) * C)
-            if s == 0:
-                h_banks[e] = psum.tile([P, H], F32, name="h_bank")
-            plane = (e * PASSES + s) * H
-            nc.tensor.matmul_mx(
-                out=h_banks[e][:], lhsT=gw[1][s][:, slots].bitcast(FP8X4), lhsT_scale=partner_scales[s][:, slots],
-                rhs=wp[e][:, s, :].bitcast(FP4X4), rhs_scale=wps[:, plane : plane + H], start=(s == 0), stop=stop,
-            )
-
-        def w1_pass(e, s):
-            slots = slice(e * C, (e + 1) * C)
-            grouped = ring.tile([P, H * PACK], BF16, name="grouped", bufs=4, align_bytes=64)
-            for h in range(2):
-                copy_on(
-                    h == 0 or e == 0,
-                    grouped[:, h * HALF * PACK : (h + 1) * HALF * PACK].rearrange("p (c i j) -> p c j i", i=4, j=PACK),
-                    w1_raw[e][s][:, :, h * HALF : (h + 1) * HALF].rearrange("p j (c i) -> p c j i", i=4),
+            for s in passes:
+                g = e * PASSES + s
+                nc.tensor.matmul_mx(
+                    out=h_banks[e][:], lhsT=gw[1][s][:, slots].bitcast(FP8X4), lhsT_scale=partner_scales[s][:, slots],
+                    rhs=wp[g].bitcast(FP4X4), rhs_scale=wps[:, g * H : (g + 1) * H],
+                    start=(s == 0), stop=stop,
                 )
+
+        def cast_w1(e, s):
+            grouped = ring.tile([P, H * PACK], BF16, name="grouped", bufs=4, align_bytes=64)
+            dst = grouped[:].rearrange("p (c i j) -> p c j i", i=4, j=PACK)
+            src = w1_raw[e, s].rearrange("p j (c i) -> p c j i", i=4)
+            share = P if (e, s) < (1, 1) else SHARE_LAST if (e, s) == (last, PASSES - 1) else SHARE_W1
+            nc.scalar.copy(out=dst[:, 0:share], in_=src[:, 0:share])
+            if share < P:
+                nc.vector.tensor_copy(out=dst[:, share:P], in_=src[:, share:P])
+            return grouped
+
+        def w1_pass(e, s, grouped):
+            slots = slice(e * C, (e + 1) * C)
             codes = ring.tile([P, H], U32, name="w1c", align_bytes=64)
             scales = ring.tile([P, H], U8, name="w1s", align_bytes=64)
             nc.vector.quantize_mx(out=codes[:].bitcast(FP8X4), scales=scales[:], in_=grouped[:])
@@ -152,117 +166,161 @@ def tile_moe_duo_s_none_kernel(
                 rhs=codes[:].bitcast(FP8X4), rhs_scale=scales[:], start=False, stop=(s == PASSES - 1 and e > 0),
             )
 
-        def spent(raw):
-            return raw[:, 0, 0:HALF].bitcast(BF16)
+        def spent_end(raw):
+            return raw[:, PACK - 1, HALF:]
 
-        def turn_h(e, pairs):
+        def spent_start(raw):
+            return raw[:, 0, 0:HALF]
+
+        def spent_row(raw):
+            return raw[:, 1, :].rearrange("p (t s) -> p t s", t=PACK)
+
+        def turn_h(e, words):
+            pairs = words.rearrange("s (u p) -> s u p", u=2)
             nc.scalar.copy(
-                out=pairs.rearrange("s (u p d) -> s u p d", u=2, d=2),
+                out=pairs.bitcast(BF16).rearrange("s u (p d) -> s u p d", d=2),
                 in_=h_banks[e][:].rearrange("s (p u d) -> s u p d", u=2, d=2),
             )
             bank = psum.tile([P, 2, C], F32, name="turned")
             turned[e] = bank
             for u in range(2):
-                nc.tensor.transpose(bank[:, u, :], pairs.bitcast(F32)[:, u * P : (u + 1) * P], ident[:])
+                nc.tensor.transpose(bank[:, u, :], pairs[:, u, :], ident[:])
 
         def quantise_h(e, grouped):
             nc.scalar.copy(
                 out=grouped.bitcast(F32).rearrange("p (s u) -> p s u", u=2),
                 in_=turned[e][:].rearrange("p u s -> p s u"),
             )
-            codes = ring.tile([P, C], U32, name="hc", align_bytes=64)
-            scales = ring.tile([P, C], U8, name="hs", align_bytes=64)
+            codes = keep.tile([P, C], U32, name="w2t1" if e == last else "hc%d" % e, align_bytes=64)
+            scales = keep.tile([P, C], U8, name="hs%d" % e, align_bytes=64)
             nc.vector.quantize_mx(out=codes[:].bitcast(FP8X4), scales=scales[:], in_=grouped)
             h_quant[e] = (codes, scales)
 
+        def cast_w2(grouped, raw, share):
+            dst = grouped.rearrange("p t (m j) -> p m j t", j=PACK)
+            src = raw.rearrange("p j (m t) -> p m j t", t=PACK)
+            width = dst.shape[1]
+            if share:
+                nc.scalar.copy(out=dst[:, 0:share], in_=src[:, 0:share])
+            nc.vector.tensor_copy(out=dst[:, share:width], in_=src[:, share:width])
+
         def open_w2(e):
-            grouped = ring.tile([P, PACK, P * PACK], BF16, name="grouped", bufs=4, align_bytes=64)
             codes = ring.tile([P, N], U32, name="w2c", align_bytes=64)
             scales = ring.tile([P, N], U8, name="w2s", align_bytes=64)
             w2_quant[e] = (codes, scales)
-            return grouped
+            return codes, scales
 
-        def w2_views(grouped, raw, h):
-            dst = grouped[:, :, h * HALF : (h + 1) * HALF].rearrange("p t (m j) -> p m j t", j=PACK)
-            return dst, raw.rearrange("p j (m t) -> p m j t", t=PACK)
-
-        def quantise_w2(e):
-            grouped = open_w2(e)
-            for h in range(2):
-                dst, src = w2_views(grouped, w2_raw[e][:, :, h * HALF : (h + 1) * HALF], h)
-                copy_on(h == 0, dst, src)
-            codes, scales = w2_quant[e]
+        def quantise_w2(e, share=SHARE_W2):
+            grouped = ring.tile([P, PACK, P * PACK], BF16, name="grouped", bufs=4, align_bytes=64)
+            cast_w2(grouped[:], w2_raw[e][:], share)
+            codes, scales = open_w2(e)
             nc.vector.quantize_mx(out=codes[:].bitcast(FP8X4), scales=scales[:], in_=grouped[:].rearrange("p t c -> p (t c)"))
 
-        def quantise_w2_half(grouped, h):
-            dst, src = w2_views(grouped, w2_tail[h][:], h)
-            share = SCALAR_SHARE if h == 0 else 0
-            if share:
-                nc.scalar.copy(out=dst[:, 0:share], in_=src[:, 0:share])
-            nc.vector.tensor_copy(out=dst[:, share:64], in_=src[:, share:64])
-            codes, scales = w2_quant[last]
-            for t in range(PACK):
-                words = slice(t * P + h * 64, t * P + (h + 1) * 64)
+        def cast_w2_half(grouped, h, share):
+            cast_w2(grouped[:, :, h * HALF : (h + 1) * HALF], w2_tail[h][:], share)
+
+        def quantise_last_w2(grouped):
+            codes, scales = open_w2(last)
+            for pair in range(2):
+                words = slice(pair * HALF, (pair + 1) * HALF)
                 nc.vector.quantize_mx(
                     out=codes[:, words].bitcast(FP8X4), scales=scales[:, words],
-                    in_=grouped[:, t, h * HALF : (h + 1) * HALF],
+                    in_=grouped[:, 2 * pair : 2 * pair + 2, :].rearrange("p t c -> p (t c)"),
                 )
 
-        def second_layer(e, staged):
+        def second_layer(e):
             codes, scales = w2_quant[e]
             hc, hs = h_quant[e]
-            banks = [psum.tile([P, PACK, C], F32, name="y_bank", bufs=3) for i in range(2 if e == last else 1)]
+            bank = psum.tile([P, PACK, C], F32, name="y_bank", bufs=4)
             for t in range(PACK):
                 words = slice(t * P, (t + 1) * P)
                 nc.tensor.matmul_mx(
-                    out=banks[t * len(banks) // PACK][:, t, :], lhsT=codes[:, words].bitcast(FP8X4), lhsT_scale=scales[:, words],
+                    out=bank[:, t, :], lhsT=codes[:, words].bitcast(FP8X4), lhsT_scale=scales[:, words],
                     rhs=hc[:].bitcast(FP8X4), rhs_scale=hs[:], start=True, stop=True,
                 )
-            slots = slice(e * C, (e + 1) * C)
-            grouped = ring.tile([P, C * PACK], BF16, name="y_grouped", align_bytes=64)
-            if e < last:
-                nc.scalar.copy(out=staged, in_=banks[0][:])
-            else:
-                nc.scalar.copy(out=staged[:, 0:2, :], in_=banks[0][:, 0:2, :])
-                nc.vector.tensor_copy(out=staged[:, 2:4, :], in_=banks[1][:, 2:4, :])
-            nc.vector.tensor_copy(out=grouped[:].rearrange("p (s t) -> p s t", t=PACK), in_=staged.rearrange("p t s -> p s t"))
-            nc.vector.quantize_mx(out=y_codes[:, slots].bitcast(FP8X4), scales=y_scales[:, slots], in_=grouped[:])
+            return bank
+
+        def stage_y(e, bank, staged):
+            nc.scalar.copy(out=staged, in_=bank[:])
             y_staged[e] = staged
 
-        partner_pass(0, 0)
-        for e in range(E):
-            w1_pass(e, 0)
-            if e >= 1:
-                turn_h(e - 1, spent(w1_raw[e][0]))
-            if e >= 2:
-                quantise_w2(e - 2)
-                quantise_h(e - 1, spent(w2_raw[e - 2]))
-            w1_pass(e, 1)
-            if e == 0:
-                partner_pass(0, 1, stop=True)
-            if e == 1:
-                quantise_h(0, spent(w1_raw[1][1]))
-            if e >= 2:
-                second_layer(e - 2, w1_raw[e][1][:, :, 0:C])
-            if e < last:
-                partner_pass(e + 1, 0)
-                partner_pass(e + 1, 1)
-        quantise_w2(last - 1)
-        turn_h(last, spent(w2_raw[last - 1]))
-        tail_grouped = open_w2(last)
-        quantise_w2_half(tail_grouped, 0)
-        h_tail = keep.tile([P, C * PACK], BF16, name="h_tail", align_bytes=64)
-        quantise_h(last, h_tail[:])
-        y_tail = [keep.tile([P, PACK, C], F32, name="y_tail%d" % i) for i in range(2)]
-        second_layer(last - 1, y_tail[0][:])
-        quantise_w2_half(tail_grouped, 1)
-        second_layer(last, y_tail[1][:])
+        def round_y(grouped, values):
+            nc.vector.tensor_copy(out=grouped.rearrange("p (s t) -> p s t", t=PACK), in_=values.rearrange("p t s -> p s t"))
+
+        def quantise_y(first, count, grouped):
+            slots = slice(first * C, (first + count) * C)
+            nc.vector.quantize_mx(out=y_codes[:, slots].bitcast(FP8X4), scales=y_scales[:, slots], in_=grouped)
+
+        def fresh_bf16(name):
+            tile = keep.tile([P, C * PACK], BF16, name=name, align_bytes=64)
+            return tile[:]
+
+        def open_h(e):
+            h_banks[e] = psum.tile([P, H], F32, name="h_bank")
+
+        def first_pass(e, s):
+            w1_pass(e, s, cast_w1(e, s))
+
+        def planes_of(e, grouped):
+            round_y(grouped, y_staged[e])
+            quantise_y(e, 1, grouped)
+
+        open_h(0)
+        partner_passes(0, (0,))
+        first_pass(0, 0)
+        first_pass(0, 1)
+        partner_passes(0, (1,), stop=True)
+        open_h(1)
+        partner_passes(1)
+        first_pass(1, 0)
+        first_pass(1, 1)
+        turn_h(0, spent_end(w1_raw[1, 1]))
+        open_h(2)
+        partner_passes(2)
+        quantise_w2(0)
+        quantise_h(0, spent_end(w2_raw[0]).bitcast(BF16))
+        turn_h(1, spent_start(w2_raw[0]))
+        y_banks[0] = second_layer(0)
+        first_pass(2, 0)
+        quantise_h(1, spent_end(w1_raw[2, 0]).bitcast(BF16))
+        stage_y(0, y_banks[0], spent_row(w1_raw[2, 0]))
+        quantise_w2(1)
+        planes_of(0, spent_end(w2_raw[1]).bitcast(BF16))
+        y_banks[1] = second_layer(1)
+        first_pass(2, 1)
+        stage_y(1, y_banks[1], spent_row(w1_raw[2, 1]))
+        open_h(last)
+        partner_passes(last)
+        first_pass(last, 0)
+        planes_of(1, spent_end(w1_raw[last, 0]).bitcast(BF16))
+        turn_h(2, spent_start(w1_raw[last, 0]))
+        first_pass(last, 1)
+        quantise_h(2, spent_end(w1_raw[last, 1]).bitcast(BF16))
+        quantise_w2(2, SHARE_F)
+        turn_h(last, spent_start(w2_raw[2]))
+        y_banks[2] = second_layer(2)
+        tail_grouped = keep.tile([P, PACK, P * PACK], BF16, name="tail_grouped", align_bytes=64)
+        cast_w2_half(tail_grouped, 0, SHARE_A)
+        cast_w2_half(tail_grouped, 1, SHARE_B)
+        quantise_h(last, fresh_bf16("h_last"))
+        quantise_last_w2(tail_grouped)
+        y_two = keep.tile([P, PACK, C], F32, name="h_last", align_bytes=64)
+        stage_y(2, y_banks[2], y_two[:])
+        for_planes = second_layer(last)
+        for_values = second_layer(last)
+        y_pair = keep.tile([P, 2, C * PACK], BF16, name="tail_grouped", align_bytes=64)
+        round_y(y_pair[:, 0, :], y_staged[2])
+        quantise_y(2, 1, y_pair[:, 0, :])
+        round_y(y_pair[:, 1, :], for_planes[:])
+        y_tail = keep.tile([P, PACK, C], F32, name="y_tail")
+        stage_y(last, for_values, y_tail[:])
+        quantise_y(last, 1, y_pair[:, 1, :])
 
         for e in range(last):
             nc.sync.dma_start(out=out0[:, :, e * C : (e + 1) * C], in_=y_staged[e])
-        nc.sync.dma_start(out=out1[:, 0 : last * C], in_=y_codes[:, 0 : last * C].bitcast(I32))
+        nc.sync.dma_start(out=out1[:, 0 : 2 * C], in_=y_codes[:, 0 : 2 * C].bitcast(I32))
         nc.scalar.dma_start(out=out0[:, :, last * C : SLOTS], in_=y_staged[last])
-        nc.sync.dma_start(out=out1[:, last * C : SLOTS], in_=y_codes[:, last * C : SLOTS].bitcast(I32))
+        nc.sync.dma_start(out=out1[:, 2 * C : SLOTS], in_=y_codes[:, 2 * C : SLOTS].bitcast(I32))
         for q in range(4):
             nc.sync.dma_start(
                 out=out_2[0, 4 * q : 4 * q + 4, :].bitcast(I32),

@@ -21,12 +21,12 @@ HALF = 256
 WINDOW = 768
 FLOPS = 2 * SLOTS * (2 * K * H + H * N)
 MERGED = ()
-SHARE_LAST = 48
-SHARE_F = 36
+SHARE_LAST = 44
+SHARE_F = 0
 SHARE_W1 = 64
 SHARE_W2 = 64
-SHARE_A = 36
-SHARE_B = 0
+SHARE_A = 44
+SHARE_B = 20
 
 
 def tile_moe_duo_s_none_kernel(
@@ -43,8 +43,7 @@ def tile_moe_duo_s_none_kernel(
         xw = keep.tile([P, T + WINDOW], U32, name="xw", align_bytes=64)
         xs = keep.tile([P, WINDOW], U8, name="xs", align_bytes=64)
         wps = keep.tile([P, E * PASSES * H], U8, name="wps", align_bytes=64)
-        wp_all = keep.tile([P, E * PASSES, 2 * H], U8, name="wp_all", align_bytes=64)
-        wp = [wp_all[:, g, :] for g in range(E * PASSES)]
+        wp = [keep.tile([P, PASSES, 2 * H], U8, name="wp%d" % e, align_bytes=64) for e in range(E)]
         w1_both = {e: keep.tile([P, PASSES, PACK, H], F32, name="w1r%d" % e, align_bytes=64) for e in MERGED}
         w1_one = {
             (e, s): keep.tile([P, PACK, H], F32, name="w1r%d_%d" % (e, s), align_bytes=64)
@@ -73,6 +72,9 @@ def tile_moe_duo_s_none_kernel(
                 for s in passes:
                     nc.sync.dma_start(out=w1_one[e, s][:].rearrange("p j c -> p (j c)"), in_=src[:, s])
 
+        def load_wp(e):
+            nc.sync.dma_start(out=wp[e][:].bitcast(I32), in_=wp_words[e].bitcast(I32).rearrange("s p c -> p s c"))
+
         def load_w2(e):
             src = w2[e].rearrange("(p j) c -> p j c", j=PACK)
             if e < last:
@@ -98,7 +100,8 @@ def tile_moe_duo_s_none_kernel(
         for r in range(4):
             nc.sync.dma_start(out=wps_dst[r:P:32], in_=wps_src[r])
         load_w1(1, (0,))
-        nc.sync.dma_start(out=wp_all[:].bitcast(I32), in_=wp_words.bitcast(I32).rearrange("e s p c -> p (e s) c"))
+        for e in range(last):
+            load_wp(e)
         load_w1(1, (1,))
 
         gw = [[keep.tile([P, SLOTS], U32, name="gw%d_%d" % (a, s), align_bytes=64) for s in range(PASSES)] for a in range(2)]
@@ -126,6 +129,7 @@ def tile_moe_duo_s_none_kernel(
         load_w2(1)
         load_w1(2, (1,))
         load_w1(last)
+        load_wp(last)
         load_w2(2)
         load_w2(last)
 
@@ -142,15 +146,15 @@ def tile_moe_duo_s_none_kernel(
                 g = e * PASSES + s
                 nc.tensor.matmul_mx(
                     out=h_banks[e][:], lhsT=gw[1][s][:, slots].bitcast(FP8X4), lhsT_scale=partner_scales[s][:, slots],
-                    rhs=wp[g].bitcast(FP4X4), rhs_scale=wps[:, g * H : (g + 1) * H],
-                    start=(s == 0), stop=stop,
+                    rhs=wp[e][:, s, :].bitcast(FP4X4), rhs_scale=wps[:, g * H : (g + 1) * H],
+                    start=(s == 0 and e < last), stop=stop,
                 )
 
         def cast_w1(e, s):
             grouped = ring.tile([P, H * PACK], BF16, name="grouped", bufs=4, align_bytes=64)
             dst = grouped[:].rearrange("p (c i j) -> p c j i", i=4, j=PACK)
             src = w1_raw[e, s].rearrange("p j (c i) -> p c j i", i=4)
-            share = P if (e, s) < (1, 1) else SHARE_LAST if (e, s) == (last, PASSES - 1) else SHARE_W1
+            share = P if (e, s) < (1, 1) else SHARE_LAST if e == last else SHARE_W1
             nc.scalar.copy(out=dst[:, 0:share], in_=src[:, 0:share])
             if share < P:
                 nc.vector.tensor_copy(out=dst[:, share:P], in_=src[:, share:P])
@@ -163,7 +167,7 @@ def tile_moe_duo_s_none_kernel(
             nc.vector.quantize_mx(out=codes[:].bitcast(FP8X4), scales=scales[:], in_=grouped[:])
             nc.tensor.matmul_mx(
                 out=h_banks[e][:], lhsT=gw[0][s][:, slots].bitcast(FP8X4), lhsT_scale=gs[0][4 * s : P, slots],
-                rhs=codes[:].bitcast(FP8X4), rhs_scale=scales[:], start=False, stop=(s == PASSES - 1 and e > 0),
+                rhs=codes[:].bitcast(FP8X4), rhs_scale=scales[:], start=(s == 0 and e == last), stop=(s == PASSES - 1 and e > 0),
             )
 
         def spent_end(raw):
@@ -172,8 +176,6 @@ def tile_moe_duo_s_none_kernel(
         def spent_start(raw):
             return raw[:, 0, 0:HALF]
 
-        def spent_row(raw):
-            return raw[:, 1, :].rearrange("p (t s) -> p t s", t=PACK)
 
         def turn_h(e, words):
             pairs = words.rearrange("s (u p) -> s u p", u=2)
@@ -191,7 +193,7 @@ def tile_moe_duo_s_none_kernel(
                 out=grouped.bitcast(F32).rearrange("p (s u) -> p s u", u=2),
                 in_=turned[e][:].rearrange("p u s -> p s u"),
             )
-            codes = keep.tile([P, C], U32, name="w2t1" if e == last else "hc%d" % e, align_bytes=64)
+            codes = keep.tile([P, C], U32, name="late" if e == last else "hc%d" % e, align_bytes=64)
             scales = keep.tile([P, C], U8, name="hs%d" % e, align_bytes=64)
             nc.vector.quantize_mx(out=codes[:].bitcast(FP8X4), scales=scales[:], in_=grouped)
             h_quant[e] = (codes, scales)
@@ -211,7 +213,10 @@ def tile_moe_duo_s_none_kernel(
             return codes, scales
 
         def quantise_w2(e, share=SHARE_W2):
-            grouped = ring.tile([P, PACK, P * PACK], BF16, name="grouped", bufs=4, align_bytes=64)
+            if e == last - 1:
+                grouped = keep.tile([P, PACK, P * PACK], BF16, name="late", align_bytes=64)
+            else:
+                grouped = ring.tile([P, PACK, P * PACK], BF16, name="grouped", bufs=4, align_bytes=64)
             cast_w2(grouped[:], w2_raw[e][:], share)
             codes, scales = open_w2(e)
             nc.vector.quantize_mx(out=codes[:].bitcast(FP8X4), scales=scales[:], in_=grouped[:].rearrange("p t c -> p (t c)"))
@@ -228,11 +233,12 @@ def tile_moe_duo_s_none_kernel(
                     in_=grouped[:, 2 * pair : 2 * pair + 2, :].rearrange("p t c -> p (t c)"),
                 )
 
-        def second_layer(e):
+        def second_layer(e, bank=None, slices=range(PACK)):
             codes, scales = w2_quant[e]
             hc, hs = h_quant[e]
-            bank = psum.tile([P, PACK, C], F32, name="y_bank", bufs=4)
-            for t in range(PACK):
+            if bank is None:
+                bank = psum.tile([P, PACK, C], F32, name="y_bank", bufs=4)
+            for t in slices:
                 words = slice(t * P, (t + 1) * P)
                 nc.tensor.matmul_mx(
                     out=bank[:, t, :], lhsT=codes[:, words].bitcast(FP8X4), lhsT_scale=scales[:, words],
@@ -261,8 +267,8 @@ def tile_moe_duo_s_none_kernel(
         def first_pass(e, s):
             w1_pass(e, s, cast_w1(e, s))
 
-        def planes_of(e, grouped):
-            round_y(grouped, y_staged[e])
+        def planes_of(e, grouped, values):
+            round_y(grouped, values)
             quantise_y(e, 1, grouped)
 
         open_h(0)
@@ -283,46 +289,50 @@ def tile_moe_duo_s_none_kernel(
         y_banks[0] = second_layer(0)
         first_pass(2, 0)
         quantise_h(1, spent_end(w1_raw[2, 0]).bitcast(BF16))
-        stage_y(0, y_banks[0], spent_row(w1_raw[2, 0]))
         quantise_w2(1)
-        planes_of(0, spent_end(w2_raw[1]).bitcast(BF16))
+        planes_of(0, spent_end(w2_raw[1]).bitcast(BF16), y_banks[0][:])
         y_banks[1] = second_layer(1)
         first_pass(2, 1)
-        stage_y(1, y_banks[1], spent_row(w1_raw[2, 1]))
+        first_two = w1_raw[2, 1][:, 1:3, :].rearrange("p a (b s) -> p (a b) s", b=2)
+        stage_y(0, y_banks[0], first_two[:, :, 0:C])
+        stage_y(1, y_banks[1], first_two[:, :, C : 2 * C])
         open_h(last)
-        partner_passes(last)
         first_pass(last, 0)
-        planes_of(1, spent_end(w1_raw[last, 0]).bitcast(BF16))
+        planes_of(1, spent_end(w1_raw[last, 0]).bitcast(BF16), y_staged[1])
         turn_h(2, spent_start(w1_raw[last, 0]))
+        partner_passes(last)
         first_pass(last, 1)
         quantise_h(2, spent_end(w1_raw[last, 1]).bitcast(BF16))
         quantise_w2(2, SHARE_F)
-        turn_h(last, spent_start(w2_raw[2]))
+        pairs_last = keep.tile([P, HALF], F32, name="pairs_last")
+        turn_h(last, pairs_last[:])
         y_banks[2] = second_layer(2)
         tail_grouped = keep.tile([P, PACK, P * PACK], BF16, name="tail_grouped", align_bytes=64)
+        quantise_h(last, fresh_bf16("h_last"))
         cast_w2_half(tail_grouped, 0, SHARE_A)
         cast_w2_half(tail_grouped, 1, SHARE_B)
-        quantise_h(last, fresh_bf16("h_last"))
         quantise_last_w2(tail_grouped)
-        y_two = keep.tile([P, PACK, C], F32, name="h_last", align_bytes=64)
-        stage_y(2, y_banks[2], y_two[:])
-        for_planes = second_layer(last)
-        for_values = second_layer(last)
+        stage_y(2, y_banks[2], w2_tail[1][:, :, 0:C])
+        for_planes = second_layer(last, slices=(0, 1))
+        for_values = [second_layer(last, slices=(0, 1))]
+        second_layer(last, for_planes, (2, 3))
+        for_values.append(second_layer(last, slices=(2, 3)))
         y_pair = keep.tile([P, 2, C * PACK], BF16, name="tail_grouped", align_bytes=64)
         round_y(y_pair[:, 0, :], y_staged[2])
-        quantise_y(2, 1, y_pair[:, 0, :])
         round_y(y_pair[:, 1, :], for_planes[:])
-        y_tail = keep.tile([P, PACK, C], F32, name="y_tail")
-        stage_y(last, for_values, y_tail[:])
-        quantise_y(last, 1, y_pair[:, 1, :])
+        last_two = w2_tail[1]
+        for pair in range(2):
+            nc.scalar.copy(out=last_two[:, 2 * pair : 2 * pair + 2, C : 2 * C], in_=for_values[pair][:, 2 * pair : 2 * pair + 2, :])
+        quantise_y(2, 2, y_pair[:].rearrange("p e c -> p (e c)"))
 
-        for e in range(last):
-            nc.sync.dma_start(out=out0[:, :, e * C : (e + 1) * C], in_=y_staged[e])
+        nc.sync.dma_start(out=out0[:, :, 0 : 2 * C], in_=first_two)
         nc.sync.dma_start(out=out1[:, 0 : 2 * C], in_=y_codes[:, 0 : 2 * C].bitcast(I32))
-        nc.scalar.dma_start(out=out0[:, :, last * C : SLOTS], in_=y_staged[last])
+        nc.sync.dma_start(out=out0[:, 0:2, 2 * C : SLOTS], in_=last_two[:, 0:2, :])
+        nc.scalar.dma_start(out=out0[:, 2:4, 2 * C : SLOTS], in_=last_two[:, 2:4, :])
         nc.sync.dma_start(out=out1[:, 2 * C : SLOTS], in_=y_codes[:, 2 * C : SLOTS].bitcast(I32))
         for q in range(4):
-            nc.sync.dma_start(
+            queue = nc.sync if q < 2 else nc.scalar
+            queue.dma_start(
                 out=out_2[0, 4 * q : 4 * q + 4, :].bitcast(I32),
                 in_=y_scales[32 * q : 32 * q + 4, :].bitcast(I32),
             )

@@ -25,8 +25,7 @@ SHARE_LAST = 44
 SHARE_F = 0
 SHARE_W1 = 64
 SHARE_W2 = 64
-SHARE_A = 44
-SHARE_B = 20
+SHARE_A = 40
 
 
 def tile_moe_duo_s_none_kernel(
@@ -52,8 +51,7 @@ def tile_moe_duo_s_none_kernel(
         w1_raw = {(e, s): w1_both[e][:, s] for e in MERGED for s in range(PASSES)}
         for key in w1_one:
             w1_raw[key] = w1_one[key][:]
-        w2_raw = [keep.tile([P, PACK, N], F32, name="w2r%d" % e, align_bytes=64) for e in range(last)]
-        w2_tail = [keep.tile([P, PACK, HALF], F32, name="w2t%d" % h, align_bytes=64) for h in range(2)]
+        w2_raw = [keep.tile([P, PACK, N], F32, name="w2r%d" % e, align_bytes=64) for e in range(E)]
         xs_rows = keep.tile([P, T // 4], I32, name="xs_rows")
         moved = keep.tile([P, SLOTS], U8, name="moved", align_bytes=64)
         ident = keep.tile([P, P], F32, name="ident")
@@ -77,11 +75,7 @@ def tile_moe_duo_s_none_kernel(
 
         def load_w2(e):
             src = w2[e].rearrange("(p j) c -> p j c", j=PACK)
-            if e < last:
-                nc.sync.dma_start(out=w2_raw[e][:], in_=src)
-            else:
-                for h in range(2):
-                    nc.sync.dma_start(out=w2_tail[h][:], in_=src[:, :, h * HALF : (h + 1) * HALF])
+            nc.sync.dma_start(out=w2_raw[e][:], in_=src)
 
         nc.sync.dma_start(
             out=xw[:, 0 : PASSES * T].bitcast(I32).rearrange("p (s t) -> p s t", s=PASSES),
@@ -221,9 +215,6 @@ def tile_moe_duo_s_none_kernel(
             codes, scales = open_w2(e)
             nc.vector.quantize_mx(out=codes[:].bitcast(FP8X4), scales=scales[:], in_=grouped[:].rearrange("p t c -> p (t c)"))
 
-        def cast_w2_half(grouped, h, share):
-            cast_w2(grouped[:, :, h * HALF : (h + 1) * HALF], w2_tail[h][:], share)
-
         def quantise_last_w2(grouped):
             codes, scales = open_w2(last)
             for pair in range(2):
@@ -309,26 +300,27 @@ def tile_moe_duo_s_none_kernel(
         y_banks[2] = second_layer(2)
         tail_grouped = keep.tile([P, PACK, P * PACK], BF16, name="tail_grouped", align_bytes=64)
         quantise_h(last, fresh_bf16("h_last"))
-        cast_w2_half(tail_grouped, 0, SHARE_A)
-        cast_w2_half(tail_grouped, 1, SHARE_B)
+        cast_w2(tail_grouped[:], w2_raw[last][:], SHARE_A)
         quantise_last_w2(tail_grouped)
-        stage_y(2, y_banks[2], w2_tail[1][:, :, 0:C])
-        for_planes = second_layer(last, slices=(0, 1))
-        for_values = [second_layer(last, slices=(0, 1))]
-        second_layer(last, for_planes, (2, 3))
-        for_values.append(second_layer(last, slices=(2, 3)))
+        stage_y(2, y_banks[2], w2_raw[last][:, :, 0:C])
+        for_values = [second_layer(last, slices=(0, 1)), second_layer(last, slices=(2, 3))]
         y_pair = keep.tile([P, 2, C * PACK], BF16, name="tail_grouped", align_bytes=64)
         round_y(y_pair[:, 0, :], y_staged[2])
-        round_y(y_pair[:, 1, :], for_planes[:])
-        last_two = w2_tail[1]
         for pair in range(2):
-            nc.scalar.copy(out=last_two[:, 2 * pair : 2 * pair + 2, C : 2 * C], in_=for_values[pair][:, 2 * pair : 2 * pair + 2, :])
+            nc.vector.tensor_copy(
+                out=y_pair[:, 1, :].rearrange("p (s t) -> p s t", t=PACK)[:, :, 2 * pair : 2 * pair + 2],
+                in_=for_values[pair][:, 2 * pair : 2 * pair + 2, :].rearrange("p t s -> p s t"),
+            )
+        last_values = keep.tile([P, PACK, C], F32, name="last_values")
+        for pair in range(2):
+            nc.scalar.copy(out=last_values[:, 2 * pair : 2 * pair + 2, :], in_=for_values[pair][:, 2 * pair : 2 * pair + 2, :])
         quantise_y(2, 2, y_pair[:].rearrange("p e c -> p (e c)"))
 
         nc.sync.dma_start(out=out0[:, :, 0 : 2 * C], in_=first_two)
         nc.sync.dma_start(out=out1[:, 0 : 2 * C], in_=y_codes[:, 0 : 2 * C].bitcast(I32))
-        nc.sync.dma_start(out=out0[:, 0:2, 2 * C : SLOTS], in_=last_two[:, 0:2, :])
-        nc.scalar.dma_start(out=out0[:, 2:4, 2 * C : SLOTS], in_=last_two[:, 2:4, :])
+        nc.sync.dma_start(out=out0[:, :, 2 * C : 3 * C], in_=y_staged[2])
+        nc.sync.dma_start(out=out0[:, 0:2, 3 * C : SLOTS], in_=last_values[:, 0:2, :])
+        nc.scalar.dma_start(out=out0[:, 2:4, 3 * C : SLOTS], in_=last_values[:, 2:4, :])
         nc.sync.dma_start(out=out1[:, 2 * C : SLOTS], in_=y_codes[:, 2 * C : SLOTS].bitcast(I32))
         for q in range(4):
             queue = nc.sync if q < 2 else nc.scalar

@@ -25,7 +25,7 @@ SHARE_LAST = 44
 SHARE_F = 0
 SHARE_W1 = 64
 SHARE_W2 = 64
-SHARE_A = 40
+SHARE_A = 96
 
 
 def tile_moe_duo_s_none_kernel(
@@ -300,27 +300,30 @@ def tile_moe_duo_s_none_kernel(
         y_banks[2] = second_layer(2)
         tail_grouped = keep.tile([P, PACK, P * PACK], BF16, name="tail_grouped", align_bytes=64)
         quantise_h(last, fresh_bf16("h_last"))
-        cast_w2(tail_grouped[:], w2_raw[last][:], SHARE_A)
+        tail_dst = tail_grouped[:].rearrange("p t (m j) -> p m j t", j=PACK)
+        tail_src = w2_raw[last][:].rearrange("p j (m t) -> p m j t", t=PACK)
+        nc.scalar.copy(out=tail_dst[:, 0:SHARE_A, :, 2:4], in_=tail_src[:, 0:SHARE_A, :, 2:4])
+        nc.vector.tensor_copy(out=tail_dst[:, :, :, 0:2], in_=tail_src[:, :, :, 0:2])
+        nc.vector.tensor_copy(out=tail_dst[:, SHARE_A:P, :, 2:4], in_=tail_src[:, SHARE_A:P, :, 2:4])
         quantise_last_w2(tail_grouped)
-        stage_y(2, y_banks[2], w2_raw[last][:, :, 0:C])
-        for_values = [second_layer(last, slices=(0, 1)), second_layer(last, slices=(2, 3))]
-        y_pair = keep.tile([P, 2, C * PACK], BF16, name="tail_grouped", align_bytes=64)
-        round_y(y_pair[:, 0, :], y_staged[2])
-        for pair in range(2):
-            nc.vector.tensor_copy(
-                out=y_pair[:, 1, :].rearrange("p (s t) -> p s t", t=PACK)[:, :, 2 * pair : 2 * pair + 2],
-                in_=for_values[pair][:, 2 * pair : 2 * pair + 2, :].rearrange("p t s -> p s t"),
-            )
+        y2_rounded = spent_start(w2_raw[last]).bitcast(BF16)
+        nc.scalar.copy(out=y2_rounded.rearrange("p (s t) -> p s t", t=PACK), in_=y_banks[2][:].rearrange("p t s -> p s t"))
+        quantise_y(2, 1, y2_rounded)
+        stage_y(2, y_banks[2], w2_raw[last][:, 1, :].rearrange("p (t s) -> p t s", t=PACK))
+        for_planes = second_layer(last)
+        for_values = [second_layer(last, slices=(2 + u, u)) for u in range(2)]
+        y_last = fresh_bf16("y_last")
+        round_y(y_last, for_planes[:])
         last_values = keep.tile([P, PACK, C], F32, name="last_values")
         for pair in range(2):
-            nc.scalar.copy(out=last_values[:, 2 * pair : 2 * pair + 2, :], in_=for_values[pair][:, 2 * pair : 2 * pair + 2, :])
-        quantise_y(2, 2, y_pair[:].rearrange("p e c -> p (e c)"))
+            nc.scalar.copy(out=last_values[:, 2 * pair : 2 * pair + 2, :], in_=for_values[pair][:, pair:PACK:2, :])
+        quantise_y(last, 1, y_last)
 
         nc.sync.dma_start(out=out0[:, :, 0 : 2 * C], in_=first_two)
         nc.sync.dma_start(out=out1[:, 0 : 2 * C], in_=y_codes[:, 0 : 2 * C].bitcast(I32))
         nc.sync.dma_start(out=out0[:, :, 2 * C : 3 * C], in_=y_staged[2])
-        nc.sync.dma_start(out=out0[:, 0:2, 3 * C : SLOTS], in_=last_values[:, 0:2, :])
-        nc.scalar.dma_start(out=out0[:, 2:4, 3 * C : SLOTS], in_=last_values[:, 2:4, :])
+        nc.sync.dma_start(out=out0[:, 0:PACK:2, 3 * C : SLOTS], in_=last_values[:, 0:2, :])
+        nc.scalar.dma_start(out=out0[:, 1:PACK:2, 3 * C : SLOTS], in_=last_values[:, 2:4, :])
         nc.sync.dma_start(out=out1[:, 2 * C : SLOTS], in_=y_codes[:, 2 * C : SLOTS].bitcast(I32))
         for q in range(4):
             queue = nc.sync if q < 2 else nc.scalar

@@ -25,7 +25,8 @@ SHARE_LAST = 44
 SHARE_F = 0
 SHARE_W1 = 64
 SHARE_W2 = 64
-SHARE_A = 96
+SHARE_A = 88
+SHARE_H = 44
 
 
 def tile_moe_duo_s_none_kernel(
@@ -173,10 +174,13 @@ def tile_moe_duo_s_none_kernel(
 
         def turn_h(e, words):
             pairs = words.rearrange("s (u p) -> s u p", u=2)
-            nc.scalar.copy(
-                out=pairs.bitcast(BF16).rearrange("s u (p d) -> s u p d", d=2),
-                in_=h_banks[e][:].rearrange("s (p u d) -> s u p d", u=2, d=2),
-            )
+            dst = pairs.bitcast(BF16).rearrange("s u (p d) -> s u p d", d=2)
+            src = h_banks[e][:].rearrange("s (p u d) -> s u p d", u=2, d=2)
+            if e == last:
+                for u in range(2):
+                    nc.scalar.copy(out=dst[:, u], in_=src[:, u])
+            else:
+                nc.scalar.copy(out=dst, in_=src)
             bank = psum.tile([P, 2, C], F32, name="turned")
             turned[e] = bank
             for u in range(2):
@@ -258,6 +262,28 @@ def tile_moe_duo_s_none_kernel(
         def first_pass(e, s):
             w1_pass(e, s, cast_w1(e, s))
 
+        def last_pass_in_halves():
+            grouped = ring.tile([P, H * PACK], BF16, name="grouped", bufs=4, align_bytes=64)
+            dst = grouped[:].rearrange("p (c i j) -> p c j i", i=4, j=PACK)
+            src = w1_raw[last, 1].rearrange("p j (c i) -> p c j i", i=4)
+            cut = P // 2 + SHARE_H
+            nc.scalar.copy(out=dst[:, P // 2 : cut], in_=src[:, P // 2 : cut])
+            nc.vector.tensor_copy(out=dst[:, 0 : P // 2], in_=src[:, 0 : P // 2])
+            nc.vector.tensor_copy(out=dst[:, cut:P], in_=src[:, cut:P])
+            slots = slice(last * C, SLOTS)
+            codes = ring.tile([P, H], U32, name="w1c", align_bytes=64)
+            scales = ring.tile([P, H], U8, name="w1s", align_bytes=64)
+            for half in range(2):
+                words = slice(half * HALF, (half + 1) * HALF)
+                nc.vector.quantize_mx(
+                    out=codes[:, words].bitcast(FP8X4), scales=scales[:, words],
+                    in_=grouped[:, half * HALF * PACK : (half + 1) * HALF * PACK],
+                )
+            nc.tensor.matmul_mx(
+                out=h_banks[last][:], lhsT=gw[0][1][:, slots].bitcast(FP8X4), lhsT_scale=gs[0][4:P, slots],
+                rhs=codes[:].bitcast(FP8X4), rhs_scale=scales[:], start=False, stop=True,
+            )
+
         def planes_of(e, grouped, values):
             round_y(grouped, values)
             quantise_y(e, 1, grouped)
@@ -292,7 +318,7 @@ def tile_moe_duo_s_none_kernel(
         planes_of(1, spent_end(w1_raw[last, 0]).bitcast(BF16), y_staged[1])
         turn_h(2, spent_start(w1_raw[last, 0]))
         partner_passes(last)
-        first_pass(last, 1)
+        last_pass_in_halves()
         quantise_h(2, spent_end(w1_raw[last, 1]).bitcast(BF16))
         quantise_w2(2, SHARE_F)
         pairs_last = keep.tile([P, HALF], F32, name="pairs_last")
@@ -306,18 +332,18 @@ def tile_moe_duo_s_none_kernel(
         nc.vector.tensor_copy(out=tail_dst[:, :, :, 0:2], in_=tail_src[:, :, :, 0:2])
         nc.vector.tensor_copy(out=tail_dst[:, SHARE_A:P, :, 2:4], in_=tail_src[:, SHARE_A:P, :, 2:4])
         quantise_last_w2(tail_grouped)
-        y2_rounded = spent_start(w2_raw[last]).bitcast(BF16)
-        nc.scalar.copy(out=y2_rounded.rearrange("p (s t) -> p s t", t=PACK), in_=y_banks[2][:].rearrange("p t s -> p s t"))
-        quantise_y(2, 1, y2_rounded)
         stage_y(2, y_banks[2], w2_raw[last][:, 1, :].rearrange("p (t s) -> p t s", t=PACK))
+        y_pair = w2_raw[last][:, 0, :].bitcast(BF16)
+        nc.scalar.copy(
+            out=y_pair[:, 0 : C * PACK].rearrange("p (s t) -> p s t", t=PACK), in_=y_banks[2][:].rearrange("p t s -> p s t")
+        )
         for_planes = second_layer(last)
         for_values = [second_layer(last, slices=(2 + u, u)) for u in range(2)]
-        y_last = fresh_bf16("y_last")
-        round_y(y_last, for_planes[:])
+        round_y(y_pair[:, C * PACK :], for_planes[:])
         last_values = keep.tile([P, PACK, C], F32, name="last_values")
         for pair in range(2):
             nc.scalar.copy(out=last_values[:, 2 * pair : 2 * pair + 2, :], in_=for_values[pair][:, pair:PACK:2, :])
-        quantise_y(last, 1, y_last)
+        quantise_y(2, 2, y_pair)
 
         nc.sync.dma_start(out=out0[:, :, 0 : 2 * C], in_=first_two)
         nc.sync.dma_start(out=out1[:, 0 : 2 * C], in_=y_codes[:, 0 : 2 * C].bitcast(I32))

@@ -25,7 +25,7 @@ SHARE_LAST = 44
 SHARE_F = 0
 SHARE_W1 = 64
 SHARE_W2 = 64
-SHARE_A = 88
+SHARE_A = 80
 SHARE_H = 44
 
 
@@ -215,12 +215,19 @@ def tile_moe_duo_s_none_kernel(
                 grouped = keep.tile([P, PACK, P * PACK], BF16, name="late", align_bytes=64)
             else:
                 grouped = ring.tile([P, PACK, P * PACK], BF16, name="grouped", bufs=4, align_bytes=64)
+            if e == last - 1:
+                dst = grouped[:].rearrange("p t (m j) -> p m j t", j=PACK)
+                src = w2_raw[e][:].rearrange("p j (m t) -> p m j t", t=PACK)
+                for pair in range(2):
+                    nc.vector.tensor_copy(out=dst[:, :, :, 2 * pair : 2 * pair + 2], in_=src[:, :, :, 2 * pair : 2 * pair + 2])
+                quantise_last_w2(grouped, e)
+                return
             cast_w2(grouped[:], w2_raw[e][:], share)
             codes, scales = open_w2(e)
             nc.vector.quantize_mx(out=codes[:].bitcast(FP8X4), scales=scales[:], in_=grouped[:].rearrange("p t c -> p (t c)"))
 
-        def quantise_last_w2(grouped):
-            codes, scales = open_w2(last)
+        def quantise_last_w2(grouped, e=last):
+            codes, scales = open_w2(e)
             for pair in range(2):
                 words = slice(pair * HALF, (pair + 1) * HALF)
                 nc.vector.quantize_mx(
@@ -332,18 +339,18 @@ def tile_moe_duo_s_none_kernel(
         nc.vector.tensor_copy(out=tail_dst[:, :, :, 0:2], in_=tail_src[:, :, :, 0:2])
         nc.vector.tensor_copy(out=tail_dst[:, SHARE_A:P, :, 2:4], in_=tail_src[:, SHARE_A:P, :, 2:4])
         quantise_last_w2(tail_grouped)
+        y2_rounded = spent_start(w2_raw[last]).bitcast(BF16)
+        nc.scalar.copy(out=y2_rounded.rearrange("p (s t) -> p s t", t=PACK), in_=y_banks[2][:].rearrange("p t s -> p s t"))
+        quantise_y(2, 1, y2_rounded)
         stage_y(2, y_banks[2], w2_raw[last][:, 1, :].rearrange("p (t s) -> p t s", t=PACK))
-        y_pair = w2_raw[last][:, 0, :].bitcast(BF16)
-        nc.scalar.copy(
-            out=y_pair[:, 0 : C * PACK].rearrange("p (s t) -> p s t", t=PACK), in_=y_banks[2][:].rearrange("p t s -> p s t")
-        )
         for_planes = second_layer(last)
         for_values = [second_layer(last, slices=(2 + u, u)) for u in range(2)]
-        round_y(y_pair[:, C * PACK :], for_planes[:])
+        y_last = fresh_bf16("y_last")
+        round_y(y_last, for_planes[:])
         last_values = keep.tile([P, PACK, C], F32, name="last_values")
         for pair in range(2):
             nc.scalar.copy(out=last_values[:, 2 * pair : 2 * pair + 2, :], in_=for_values[pair][:, pair:PACK:2, :])
-        quantise_y(2, 2, y_pair)
+        quantise_y(last, 1, y_last)
 
         nc.sync.dma_start(out=out0[:, :, 0 : 2 * C], in_=first_two)
         nc.sync.dma_start(out=out1[:, 0 : 2 * C], in_=y_codes[:, 0 : 2 * C].bitcast(I32))

@@ -21,10 +21,10 @@ HALF = 256
 WINDOW = 768
 FLOPS = 2 * SLOTS * (2 * K * H + H * N)
 MERGED = ()
-SHARE_LAST = 44
-SHARE_F = 0
-SHARE_W1 = 64
+SHARE_W1 = 56
 SHARE_W2 = 64
+SHARE_B = 40
+SHARE_C = 48
 SHARE_A = 80
 SHARE_H = 44
 
@@ -52,7 +52,10 @@ def tile_moe_duo_s_none_kernel(
         w1_raw = {(e, s): w1_both[e][:, s] for e in MERGED for s in range(PASSES)}
         for key in w1_one:
             w1_raw[key] = w1_one[key][:]
-        w2_raw = [keep.tile([P, PACK, N], F32, name="w2r%d" % e, align_bytes=64) for e in range(E)]
+        lead = PACK * 2 * C - C
+        w2_tiles = [keep.tile([P, PACK * N + (lead if e == 2 else 0)], F32, name="w2r%d" % e, align_bytes=64) for e in range(E)]
+        w2_raw = [w2_tiles[e][:, (lead if e == 2 else 0) :].rearrange("p (j c) -> p j c", j=PACK) for e in range(E)]
+        first_two = w2_tiles[2][:, 0 : PACK * 2 * C].rearrange("p (t s) -> p t s", t=PACK)
         xs_rows = keep.tile([P, T // 4], I32, name="xs_rows")
         moved = keep.tile([P, SLOTS], U8, name="moved", align_bytes=64)
         ident = keep.tile([P, P], F32, name="ident")
@@ -76,7 +79,7 @@ def tile_moe_duo_s_none_kernel(
 
         def load_w2(e):
             src = w2[e].rearrange("(p j) c -> p j c", j=PACK)
-            nc.sync.dma_start(out=w2_raw[e][:], in_=src)
+            nc.sync.dma_start(out=w2_raw[e], in_=src)
 
         nc.sync.dma_start(
             out=xw[:, 0 : PASSES * T].bitcast(I32).rearrange("p (s t) -> p s t", s=PASSES),
@@ -120,13 +123,11 @@ def tile_moe_duo_s_none_kernel(
             )
         partner_scales = (gs[1], moved)
         load_w2(0)
-        load_w1(2, (0,))
-        load_w2(1)
-        load_w1(2, (1,))
+        load_w1(2)
         load_w1(last)
         load_wp(last)
-        load_w2(2)
-        load_w2(last)
+        for e in range(1, E):
+            load_w2(e)
 
         y_codes = keep.tile([P, SLOTS], U32, name="y_codes", align_bytes=64)
         y_scales = keep.tile([P, SLOTS], U8, name="y_scales", align_bytes=64)
@@ -149,7 +150,7 @@ def tile_moe_duo_s_none_kernel(
             grouped = ring.tile([P, H * PACK], BF16, name="grouped", bufs=4, align_bytes=64)
             dst = grouped[:].rearrange("p (c i j) -> p c j i", i=4, j=PACK)
             src = w1_raw[e, s].rearrange("p j (c i) -> p c j i", i=4)
-            share = P if (e, s) < (1, 1) else SHARE_LAST if e == last else SHARE_W1
+            share = P if (e, s) < (1, 1) else SHARE_W1
             nc.scalar.copy(out=dst[:, 0:share], in_=src[:, 0:share])
             if share < P:
                 nc.vector.tensor_copy(out=dst[:, share:P], in_=src[:, share:P])
@@ -186,11 +187,17 @@ def tile_moe_duo_s_none_kernel(
             for u in range(2):
                 nc.tensor.transpose(bank[:, u, :], pairs[:, u, :], ident[:])
 
-        def quantise_h(e, grouped):
+        def unturn_h(e, grouped):
             nc.scalar.copy(
                 out=grouped.bitcast(F32).rearrange("p (s u) -> p s u", u=2),
                 in_=turned[e][:].rearrange("p u s -> p s u"),
             )
+
+        def quantise_h(e, grouped):
+            unturn_h(e, grouped)
+            quantise_turned(e, grouped)
+
+        def quantise_turned(e, grouped):
             codes = keep.tile([P, C], U32, name="late" if e == last else "hc%d" % e, align_bytes=64)
             scales = keep.tile([P, C], U8, name="hs%d" % e, align_bytes=64)
             nc.vector.quantize_mx(out=codes[:].bitcast(FP8X4), scales=scales[:], in_=grouped)
@@ -210,21 +217,21 @@ def tile_moe_duo_s_none_kernel(
             w2_quant[e] = (codes, scales)
             return codes, scales
 
-        def quantise_w2(e, share=SHARE_W2):
-            if e == last - 1:
-                grouped = keep.tile([P, PACK, P * PACK], BF16, name="late", align_bytes=64)
-            else:
-                grouped = ring.tile([P, PACK, P * PACK], BF16, name="grouped", bufs=4, align_bytes=64)
-            if e == last - 1:
-                dst = grouped[:].rearrange("p t (m j) -> p m j t", j=PACK)
-                src = w2_raw[e][:].rearrange("p j (m t) -> p m j t", t=PACK)
-                for pair in range(2):
-                    nc.vector.tensor_copy(out=dst[:, :, :, 2 * pair : 2 * pair + 2], in_=src[:, :, :, 2 * pair : 2 * pair + 2])
-                quantise_last_w2(grouped, e)
-                return
-            cast_w2(grouped[:], w2_raw[e][:], share)
+        def quantise_w2(e, share):
+            grouped = ring.tile([P, PACK, P * PACK], BF16, name="grouped", bufs=4, align_bytes=64)
+            cast_w2(grouped[:], w2_raw[e], share)
             codes, scales = open_w2(e)
             nc.vector.quantize_mx(out=codes[:].bitcast(FP8X4), scales=scales[:], in_=grouped[:].rearrange("p t c -> p (t c)"))
+
+        def cast_by_slices(e, grouped, share):
+            dst = grouped[:].rearrange("p t (m j) -> p m j t", j=PACK)
+            src = w2_raw[e].rearrange("p j (m t) -> p m j t", t=PACK)
+            nc.scalar.copy(out=dst[:, 0:share, :, 2:4], in_=src[:, 0:share, :, 2:4])
+            nc.vector.tensor_copy(out=dst[:, :, :, 0:2], in_=src[:, :, :, 0:2])
+            nc.vector.tensor_copy(out=dst[:, share:P, :, 2:4], in_=src[:, share:P, :, 2:4])
+
+        def round_y_on_scalar(grouped, bank):
+            nc.scalar.copy(out=grouped.rearrange("p (s t) -> p s t", t=PACK), in_=bank[:].rearrange("p t s -> p s t"))
 
         def quantise_last_w2(grouped, e=last):
             codes, scales = open_w2(e)
@@ -307,40 +314,40 @@ def tile_moe_duo_s_none_kernel(
         turn_h(0, spent_end(w1_raw[1, 1]))
         open_h(2)
         partner_passes(2)
-        quantise_w2(0)
+        quantise_w2(0, SHARE_W2)
         quantise_h(0, spent_end(w2_raw[0]).bitcast(BF16))
         turn_h(1, spent_start(w2_raw[0]))
         y_banks[0] = second_layer(0)
         first_pass(2, 0)
         quantise_h(1, spent_end(w1_raw[2, 0]).bitcast(BF16))
-        quantise_w2(1)
-        planes_of(0, spent_end(w2_raw[1]).bitcast(BF16), y_banks[0][:])
-        y_banks[1] = second_layer(1)
         first_pass(2, 1)
-        first_two = w1_raw[2, 1][:, 1:3, :].rearrange("p a (b s) -> p (a b) s", b=2)
         stage_y(0, y_banks[0], first_two[:, :, 0:C])
-        stage_y(1, y_banks[1], first_two[:, :, C : 2 * C])
         open_h(last)
         first_pass(last, 0)
-        planes_of(1, spent_end(w1_raw[last, 0]).bitcast(BF16), y_staged[1])
+        planes_of(0, spent_end(w1_raw[last, 0]).bitcast(BF16), y_staged[0])
         turn_h(2, spent_start(w1_raw[last, 0]))
         partner_passes(last)
         last_pass_in_halves()
         quantise_h(2, spent_end(w1_raw[last, 1]).bitcast(BF16))
-        quantise_w2(2, SHARE_F)
-        pairs_last = keep.tile([P, HALF], F32, name="pairs_last")
-        turn_h(last, pairs_last[:])
+        quantise_w2(1, SHARE_B)
+        turn_h(last, spent_start(w2_raw[1]))
+        y_banks[1] = second_layer(1)
+        late_grouped = keep.tile([P, PACK, P * PACK], BF16, name="late", align_bytes=64)
+        h_last = fresh_bf16("h_last")
+        unturn_h(last, h_last)
+        cast_by_slices(2, late_grouped, SHARE_C)
+        quantise_last_w2(late_grouped, 2)
+        quantise_turned(last, h_last)
+        y1_rounded = spent_end(w2_raw[2]).bitcast(BF16)
+        round_y_on_scalar(y1_rounded, y_banks[1])
+        quantise_y(1, 1, y1_rounded)
+        stage_y(1, y_banks[1], first_two[:, :, C : 2 * C])
         y_banks[2] = second_layer(2)
         tail_grouped = keep.tile([P, PACK, P * PACK], BF16, name="tail_grouped", align_bytes=64)
-        quantise_h(last, fresh_bf16("h_last"))
-        tail_dst = tail_grouped[:].rearrange("p t (m j) -> p m j t", j=PACK)
-        tail_src = w2_raw[last][:].rearrange("p j (m t) -> p m j t", t=PACK)
-        nc.scalar.copy(out=tail_dst[:, 0:SHARE_A, :, 2:4], in_=tail_src[:, 0:SHARE_A, :, 2:4])
-        nc.vector.tensor_copy(out=tail_dst[:, :, :, 0:2], in_=tail_src[:, :, :, 0:2])
-        nc.vector.tensor_copy(out=tail_dst[:, SHARE_A:P, :, 2:4], in_=tail_src[:, SHARE_A:P, :, 2:4])
+        cast_by_slices(last, tail_grouped, SHARE_A)
         quantise_last_w2(tail_grouped)
         y2_rounded = spent_start(w2_raw[last]).bitcast(BF16)
-        nc.scalar.copy(out=y2_rounded.rearrange("p (s t) -> p s t", t=PACK), in_=y_banks[2][:].rearrange("p t s -> p s t"))
+        round_y_on_scalar(y2_rounded, y_banks[2])
         quantise_y(2, 1, y2_rounded)
         stage_y(2, y_banks[2], w2_raw[last][:, 1, :].rearrange("p (t s) -> p t s", t=PACK))
         for_planes = second_layer(last)

@@ -20,13 +20,13 @@ SLOTS = E * C
 HALF = 256
 WINDOW = 768
 FLOPS = 2 * SLOTS * (2 * K * H + H * N)
-MERGED = ()
+TOKEN, PARTNER = 0, 1
+W1_LOADS = ((0, 2), (2, 4), (4, 6), (6, 7), (7, 8))
+SHARE_PAIR = 96
 SHARE_W1 = 56
-SHARE_W2 = 64
-SHARE_B = 40
-SHARE_C = 48
-SHARE_A = 80
-SHARE_H = 44
+SHARE_W2 = 56
+SHARE_SLICES = 96
+SHARE_LAST = 80
 
 
 def tile_moe_duo_s_none_kernel(
@@ -41,212 +41,155 @@ def tile_moe_duo_s_none_kernel(
 
         lists = [keep.tile([P, SLOTS // 16], U16, name="list%d" % a) for a in range(2)]
         xw = keep.tile([P, T + WINDOW], U32, name="xw", align_bytes=64)
-        xs = keep.tile([P, WINDOW], U8, name="xs", align_bytes=64)
+        xs = keep.tile([P, T + WINDOW], U8, name="xs", align_bytes=64)
         wps = keep.tile([P, E * PASSES * H], U8, name="wps", align_bytes=64)
-        wp = [keep.tile([P, PASSES, 2 * H], U8, name="wp%d" % e, align_bytes=64) for e in range(E)]
-        w1_both = {e: keep.tile([P, PASSES, PACK, H], F32, name="w1r%d" % e, align_bytes=64) for e in MERGED}
-        w1_one = {
-            (e, s): keep.tile([P, PACK, H], F32, name="w1r%d_%d" % (e, s), align_bytes=64)
-            for e in range(E) for s in range(PASSES) if e not in MERGED
-        }
-        w1_raw = {(e, s): w1_both[e][:, s] for e in MERGED for s in range(PASSES)}
-        for key in w1_one:
-            w1_raw[key] = w1_one[key][:]
-        lead = PACK * 2 * C - C
-        w2_tiles = [keep.tile([P, PACK * N + (lead if e == 2 else 0)], F32, name="w2r%d" % e, align_bytes=64) for e in range(E)]
-        w2_raw = [w2_tiles[e][:, (lead if e == 2 else 0) :].rearrange("p (j c) -> p j c", j=PACK) for e in range(E)]
-        first_two = w2_tiles[2][:, 0 : PACK * 2 * C].rearrange("p (t s) -> p t s", t=PACK)
-        xs_rows = keep.tile([P, T // 4], I32, name="xs_rows")
-        moved = keep.tile([P, SLOTS], U8, name="moved", align_bytes=64)
+        wp = keep.tile([P, E * PASSES, 2 * H], U8, name="wp", align_bytes=64)
+        w1_tiles = [keep.tile([P, b - a, PACK * H], F32, name="w1r%d" % a, align_bytes=64) for a, b in W1_LOADS]
+        w1_raw = [
+            tile[:, g - a, :].rearrange("p (j c) -> p j c", j=PACK)
+            for tile, (a, b) in zip(w1_tiles, W1_LOADS) for g in range(a, b)
+        ]
+        w2_tiles = [keep.tile([P, PACK, N], F32, name="w2r%d" % e, align_bytes=64) for e in range(E)]
         ident = keep.tile([P, P], F32, name="ident")
 
         nc.gpsimd.memset(xs[:].bitcast(I32), 0)
-        nc.vector.memset(xw[:, PASSES * T :].bitcast(I32), 0)
         nc.vector.memset(wps[:].bitcast(I32), 0)
-        nc.gpsimd.memset(moved[:].bitcast(I32), 0)
+        nc.vector.memset(xw[:, PASSES * T :].bitcast(I32), 0)
         make_identity(nc, ident[:])
 
-        def load_w1(e, passes=range(PASSES)):
-            src = w1[e].rearrange("(s p j) c -> p s (j c)", s=PASSES, j=PACK)
-            if e in MERGED:
-                nc.sync.dma_start(out=w1_both[e][:].rearrange("p s j c -> p s (j c)"), in_=src)
-            else:
-                for s in passes:
-                    nc.sync.dma_start(out=w1_one[e, s][:].rearrange("p j c -> p (j c)"), in_=src[:, s])
+        w1_src = w1.rearrange("e (s p j) c -> p (e s) (j c)", s=PASSES, j=PACK)
 
-        def load_wp(e):
-            nc.sync.dma_start(out=wp[e][:].bitcast(I32), in_=wp_words[e].bitcast(I32).rearrange("s p c -> p s c"))
+        def load_w1(n):
+            a, b = W1_LOADS[n]
+            nc.sync.dma_start(out=w1_tiles[n][:], in_=w1_src[:, a:b, :])
 
         def load_w2(e):
-            src = w2[e].rearrange("(p j) c -> p j c", j=PACK)
-            nc.sync.dma_start(out=w2_raw[e], in_=src)
+            nc.sync.dma_start(out=w2_tiles[e][:], in_=w2[e].rearrange("(p j) c -> p j c", j=PACK))
 
         nc.sync.dma_start(
             out=xw[:, 0 : PASSES * T].bitcast(I32).rearrange("p (s t) -> p s t", s=PASSES),
             in_=x_words.rearrange("s p t d -> p s (t d)").bitcast(I32),
         )
-        nc.sync.dma_start(out=lists[1][:], in_=offs2)
-        nc.sync.dma_start(out=lists[0][:], in_=offs)
-        for q in range(4):
-            nc.sync.dma_start(
-                out=xs_rows[32 * q : 32 * q + 4 * PASSES, :],
-                in_=x_scales[:, 4 * q : 4 * q + 4, :].bitcast(I32),
-            )
+        nc.sync.dma_start(out=lists[PARTNER][:], in_=offs2)
+        nc.sync.dma_start(out=lists[TOKEN][:], in_=offs)
+        xs_src = x_scales.bitcast(I32).rearrange("s (q r) c -> r q s c", r=4)
+        xs_dst = xs[:, 0 : PASSES * T].bitcast(I32).rearrange("p (s c) -> p s c", s=PASSES)
+        for r in range(4):
+            nc.sync.dma_start(out=xs_dst[r:P:32], in_=xs_src[r])
         load_w1(0)
         wps_src = wp_scales.bitcast(I32).rearrange("e s (q r) c -> r q (e s) c", r=4)
         wps_dst = wps[:].bitcast(I32).rearrange("p (g c) -> p g c", g=E * PASSES)
         for r in range(4):
             nc.sync.dma_start(out=wps_dst[r:P:32], in_=wps_src[r])
-        load_w1(1, (0,))
-        for e in range(last):
-            load_wp(e)
-        load_w1(1, (1,))
-
-        gw = [[keep.tile([P, SLOTS], U32, name="gw%d_%d" % (a, s), align_bytes=64) for s in range(PASSES)] for a in range(2)]
-        gs = [keep.tile([P, SLOTS], U8, name="gs%d" % a, align_bytes=64) for a in range(2)]
-
-        def gather_words(a):
-            for s in range(PASSES):
-                nc.vector.tensor_copy(gw[a][s][:], xw[:, s * T : s * T + WINDOW].indirect(lists[a][:]))
-
-        gather_words(1)
-        for q in range(4):
-            rows = slice(32 * q, 32 * q + 4 * PASSES)
-            nc.vector.tensor_copy(out=xs[:, 0:T].bitcast(I32)[rows, :], in_=xs_rows[rows, :])
-        nc.vector.tensor_copy(gs[1][:], xs[:].indirect(lists[1][:]))
-        gather_words(0)
-        nc.vector.tensor_copy(gs[0][:], xs[:].indirect(lists[0][:]))
-        for q in range(4):
-            nc.sync.dma_start(
-                out=moved[32 * q : 32 * q + 4, :].bitcast(I32),
-                in_=gs[1][32 * q + 4 : 32 * q + 8, :].bitcast(I32),
-            )
-        partner_scales = (gs[1], moved)
+        nc.sync.dma_start(out=wp[:].bitcast(I32), in_=wp_words.bitcast(I32).rearrange("e s p c -> p (e s) c"))
         load_w2(0)
-        load_w1(2)
-        load_w1(last)
-        load_wp(last)
+        for n in range(1, len(W1_LOADS)):
+            load_w1(n)
         for e in range(1, E):
             load_w2(e)
+
+        gw = [[keep.tile([P, SLOTS], U32, name="gw%d_%d" % (a, s), align_bytes=64) for s in range(PASSES)] for a in range(2)]
+        gs = [[keep.tile([P, SLOTS], U8, name="gs%d_%d" % (a, s), align_bytes=64) for s in range(PASSES)] for a in range(2)]
+        for a in (PARTNER, TOKEN):
+            for s in range(PASSES):
+                nc.vector.tensor_copy(gw[a][s][:], xw[:, s * T : s * T + WINDOW].indirect(lists[a][:]))
+            for s in range(PASSES):
+                nc.vector.tensor_copy(gs[a][s][:], xs[:, s * T : s * T + WINDOW].indirect(lists[a][:]))
 
         y_codes = keep.tile([P, SLOTS], U32, name="y_codes", align_bytes=64)
         y_scales = keep.tile([P, SLOTS], U8, name="y_scales", align_bytes=64)
         out0 = out_0.rearrange("(p t) j -> p t j", t=PACK)
         out1 = out_1[0].rearrange("p j d -> p (j d)").bitcast(I32)
 
-        h_banks, turned, h_quant, w2_quant, y_banks, y_staged = {}, {}, {}, {}, {}, {}
+        h_banks, turned, h_quant, w2_quant = {}, {}, {}, {}
 
-        def partner_passes(e, passes=range(PASSES), stop=False):
+        def first_layer_pass(e, s, side, rhs, rhs_scale, start, stop):
             slots = slice(e * C, (e + 1) * C)
-            for s in passes:
+            nc.tensor.matmul_mx(
+                out=h_banks[e][:], lhsT=gw[side][s][:, slots].bitcast(FP8X4), lhsT_scale=gs[side][s][:, slots],
+                rhs=rhs, rhs_scale=rhs_scale, start=start, stop=stop,
+            )
+
+        def partner_passes(e, start, stop):
+            for s in range(PASSES):
                 g = e * PASSES + s
-                nc.tensor.matmul_mx(
-                    out=h_banks[e][:], lhsT=gw[1][s][:, slots].bitcast(FP8X4), lhsT_scale=partner_scales[s][:, slots],
-                    rhs=wp[e][:, s, :].bitcast(FP4X4), rhs_scale=wps[:, g * H : (g + 1) * H],
-                    start=(s == 0 and e < last), stop=stop,
+                first_layer_pass(
+                    e, s, PARTNER, wp[:, g, :].bitcast(FP4X4), wps[:, g * H : (g + 1) * H],
+                    start and s == 0, stop and s == PASSES - 1,
                 )
 
-        def cast_w1(e, s):
-            grouped = ring.tile([P, H * PACK], BF16, name="grouped", bufs=4, align_bytes=64)
-            dst = grouped[:].rearrange("p (c i j) -> p c j i", i=4, j=PACK)
-            src = w1_raw[e, s].rearrange("p j (c i) -> p c j i", i=4)
-            share = P if (e, s) < (1, 1) else SHARE_W1
-            nc.scalar.copy(out=dst[:, 0:share], in_=src[:, 0:share])
+        def shared_cast(dst, src, share):
+            if share:
+                nc.scalar.copy(out=dst[:, 0:share], in_=src[:, 0:share])
             if share < P:
                 nc.vector.tensor_copy(out=dst[:, share:P], in_=src[:, share:P])
+
+        def cast_w1(e, s, share):
+            grouped = ring.tile([P, H * PACK], BF16, name="grouped", bufs=4, align_bytes=64)
+            dst = grouped[:].rearrange("p (c i j) -> p c j i", i=4, j=PACK)
+            src = w1_raw[e * PASSES + s].rearrange("p j (c i) -> p c j i", i=4)
+            shared_cast(dst, src, share)
             return grouped
 
-        def w1_pass(e, s, grouped):
-            slots = slice(e * C, (e + 1) * C)
+        def token_pass(e, s, grouped, start, stop):
             codes = ring.tile([P, H], U32, name="w1c", align_bytes=64)
             scales = ring.tile([P, H], U8, name="w1s", align_bytes=64)
             nc.vector.quantize_mx(out=codes[:].bitcast(FP8X4), scales=scales[:], in_=grouped[:])
-            nc.tensor.matmul_mx(
-                out=h_banks[e][:], lhsT=gw[0][s][:, slots].bitcast(FP8X4), lhsT_scale=gs[0][4 * s : P, slots],
-                rhs=codes[:].bitcast(FP8X4), rhs_scale=scales[:], start=(s == 0 and e == last), stop=(s == PASSES - 1 and e > 0),
-            )
-
-        def spent_end(raw):
-            return raw[:, PACK - 1, HALF:]
-
-        def spent_start(raw):
-            return raw[:, 0, 0:HALF]
-
+            first_layer_pass(e, s, TOKEN, codes[:].bitcast(FP8X4), scales[:], start, stop)
 
         def turn_h(e, words):
             pairs = words.rearrange("s (u p) -> s u p", u=2)
             dst = pairs.bitcast(BF16).rearrange("s u (p d) -> s u p d", d=2)
-            src = h_banks[e][:].rearrange("s (p u d) -> s u p d", u=2, d=2)
-            if e == last:
-                for u in range(2):
-                    nc.scalar.copy(out=dst[:, u], in_=src[:, u])
-            else:
-                nc.scalar.copy(out=dst, in_=src)
-            bank = psum.tile([P, 2, C], F32, name="turned")
+            nc.scalar.copy(out=dst, in_=h_banks[e][:].rearrange("s (p u d) -> s u p d", u=2, d=2))
+            bank = psum.tile([P, 2, C], F32, name="turned", bufs=1)
             turned[e] = bank
             for u in range(2):
                 nc.tensor.transpose(bank[:, u, :], pairs[:, u, :], ident[:])
 
-        def unturn_h(e, grouped):
+        def quantise_h(e, words):
             nc.scalar.copy(
-                out=grouped.bitcast(F32).rearrange("p (s u) -> p s u", u=2),
+                out=words.rearrange("p (s u) -> p s u", u=2),
                 in_=turned[e][:].rearrange("p u s -> p s u"),
             )
-
-        def quantise_h(e, grouped):
-            unturn_h(e, grouped)
-            quantise_turned(e, grouped)
-
-        def quantise_turned(e, grouped):
-            codes = keep.tile([P, C], U32, name="late" if e == last else "hc%d" % e, align_bytes=64)
+            codes = keep.tile([P, C], U32, name="hc%d" % e, align_bytes=64)
             scales = keep.tile([P, C], U8, name="hs%d" % e, align_bytes=64)
-            nc.vector.quantize_mx(out=codes[:].bitcast(FP8X4), scales=scales[:], in_=grouped)
+            nc.vector.quantize_mx(out=codes[:].bitcast(FP8X4), scales=scales[:], in_=words.bitcast(BF16))
             h_quant[e] = (codes, scales)
 
-        def cast_w2(grouped, raw, share):
-            dst = grouped.rearrange("p t (m j) -> p m j t", j=PACK)
-            src = raw.rearrange("p j (m t) -> p m j t", t=PACK)
-            width = dst.shape[1]
-            if share:
-                nc.scalar.copy(out=dst[:, 0:share], in_=src[:, 0:share])
-            nc.vector.tensor_copy(out=dst[:, share:width], in_=src[:, share:width])
+        def w2_views(e):
+            grouped = ring.tile([P, PACK, P * PACK], BF16, name="grouped", bufs=4, align_bytes=64)
+            dst = grouped[:].rearrange("p t (m j) -> p m j t", j=PACK)
+            src = w2_tiles[e][:].rearrange("p j (m t) -> p m j t", t=PACK)
+            return grouped, dst, src
 
-        def open_w2(e):
+        def quantise_w2(e, grouped, calls):
             codes = ring.tile([P, N], U32, name="w2c", align_bytes=64)
             scales = ring.tile([P, N], U8, name="w2s", align_bytes=64)
             w2_quant[e] = (codes, scales)
-            return codes, scales
+            step = PACK // calls
+            for t in range(0, PACK, step):
+                words = slice(t * P, (t + step) * P)
+                nc.vector.quantize_mx(
+                    out=codes[:, words].bitcast(FP8X4), scales=scales[:, words],
+                    in_=grouped[:, t : t + step, :].rearrange("p t c -> p (t c)"),
+                )
 
-        def quantise_w2(e, share):
-            grouped = ring.tile([P, PACK, P * PACK], BF16, name="grouped", bufs=4, align_bytes=64)
-            cast_w2(grouped[:], w2_raw[e], share)
-            codes, scales = open_w2(e)
-            nc.vector.quantize_mx(out=codes[:].bitcast(FP8X4), scales=scales[:], in_=grouped[:].rearrange("p t c -> p (t c)"))
+        def cast_w2(e, share):
+            grouped, dst, src = w2_views(e)
+            shared_cast(dst, src, share)
+            return grouped
 
-        def cast_by_slices(e, grouped, share):
-            dst = grouped[:].rearrange("p t (m j) -> p m j t", j=PACK)
-            src = w2_raw[e].rearrange("p j (m t) -> p m j t", t=PACK)
+        def cast_by_slices(e, share):
+            grouped, dst, src = w2_views(e)
             nc.scalar.copy(out=dst[:, 0:share, :, 2:4], in_=src[:, 0:share, :, 2:4])
             nc.vector.tensor_copy(out=dst[:, :, :, 0:2], in_=src[:, :, :, 0:2])
             nc.vector.tensor_copy(out=dst[:, share:P, :, 2:4], in_=src[:, share:P, :, 2:4])
+            return grouped
 
-        def round_y_on_scalar(grouped, bank):
-            nc.scalar.copy(out=grouped.rearrange("p (s t) -> p s t", t=PACK), in_=bank[:].rearrange("p t s -> p s t"))
-
-        def quantise_last_w2(grouped, e=last):
-            codes, scales = open_w2(e)
-            for pair in range(2):
-                words = slice(pair * HALF, (pair + 1) * HALF)
-                nc.vector.quantize_mx(
-                    out=codes[:, words].bitcast(FP8X4), scales=scales[:, words],
-                    in_=grouped[:, 2 * pair : 2 * pair + 2, :].rearrange("p t c -> p (t c)"),
-                )
-
-        def second_layer(e, bank=None, slices=range(PACK)):
+        def second_layer(e, slices=range(PACK)):
             codes, scales = w2_quant[e]
             hc, hs = h_quant[e]
-            if bank is None:
-                bank = psum.tile([P, PACK, C], F32, name="y_bank", bufs=4)
+            bank = psum.tile([P, PACK, C], F32, name="y_bank", bufs=4)
             for t in slices:
                 words = slice(t * P, (t + 1) * P)
                 nc.tensor.matmul_mx(
@@ -255,116 +198,94 @@ def tile_moe_duo_s_none_kernel(
                 )
             return bank
 
-        def stage_y(e, bank, staged):
-            nc.scalar.copy(out=staged, in_=bank[:])
-            y_staged[e] = staged
+        def round_y(copy, values, grouped):
+            copy(out=grouped.rearrange("p (s t) -> p s t", t=PACK), in_=values.rearrange("p t s -> p s t"))
+            return grouped
 
-        def round_y(grouped, values):
-            nc.vector.tensor_copy(out=grouped.rearrange("p (s t) -> p s t", t=PACK), in_=values.rearrange("p t s -> p s t"))
-
-        def quantise_y(first, count, grouped):
-            slots = slice(first * C, (first + count) * C)
-            nc.vector.quantize_mx(out=y_codes[:, slots].bitcast(FP8X4), scales=y_scales[:, slots], in_=grouped)
-
-        def fresh_bf16(name):
-            tile = keep.tile([P, C * PACK], BF16, name=name, align_bytes=64)
+        def fresh_rounded(e):
+            tile = keep.tile([P, C * PACK], BF16, name="y_rounded%d" % e, align_bytes=64)
             return tile[:]
 
+        def quantise_y(e, grouped):
+            slots = slice(e * C, (e + 1) * C)
+            nc.vector.quantize_mx(out=y_codes[:, slots].bitcast(FP8X4), scales=y_scales[:, slots], in_=grouped)
+
         def open_h(e):
-            h_banks[e] = psum.tile([P, H], F32, name="h_bank")
+            h_banks[e] = psum.tile([P, H], F32, name="h_bank", bufs=3)
 
-        def first_pass(e, s):
-            w1_pass(e, s, cast_w1(e, s))
+        def pair_of_passes(e, start, stop):
+            first = cast_w1(e, 0, 0)
+            second = cast_w1(e, 1, SHARE_PAIR)
+            token_pass(e, 0, first, start, False)
+            token_pass(e, 1, second, False, stop)
 
-        def last_pass_in_halves():
-            grouped = ring.tile([P, H * PACK], BF16, name="grouped", bufs=4, align_bytes=64)
-            dst = grouped[:].rearrange("p (c i j) -> p c j i", i=4, j=PACK)
-            src = w1_raw[last, 1].rearrange("p j (c i) -> p c j i", i=4)
-            cut = P // 2 + SHARE_H
-            nc.scalar.copy(out=dst[:, P // 2 : cut], in_=src[:, P // 2 : cut])
-            nc.vector.tensor_copy(out=dst[:, 0 : P // 2], in_=src[:, 0 : P // 2])
-            nc.vector.tensor_copy(out=dst[:, cut:P], in_=src[:, cut:P])
-            slots = slice(last * C, SLOTS)
-            codes = ring.tile([P, H], U32, name="w1c", align_bytes=64)
-            scales = ring.tile([P, H], U8, name="w1s", align_bytes=64)
-            for half in range(2):
-                words = slice(half * HALF, (half + 1) * HALF)
-                nc.vector.quantize_mx(
-                    out=codes[:, words].bitcast(FP8X4), scales=scales[:, words],
-                    in_=grouped[:, half * HALF * PACK : (half + 1) * HALF * PACK],
-                )
-            nc.tensor.matmul_mx(
-                out=h_banks[last][:], lhsT=gw[0][1][:, slots].bitcast(FP8X4), lhsT_scale=gs[0][4:P, slots],
-                rhs=codes[:].bitcast(FP8X4), rhs_scale=scales[:], start=False, stop=True,
-            )
+        def spent_half(raw, row):
+            return raw[:, row, HALF:]
 
-        def planes_of(e, grouped, values):
-            round_y(grouped, values)
-            quantise_y(e, 1, grouped)
+        def stage_y(bank, raw):
+            staged = raw[:, 1, :].rearrange("p (t s) -> p t s", t=PACK)
+            nc.scalar.copy(out=staged, in_=bank[:])
+            return staged
 
         open_h(0)
-        partner_passes(0, (0,))
-        first_pass(0, 0)
-        first_pass(0, 1)
-        partner_passes(0, (1,), stop=True)
-        open_h(1)
-        partner_passes(1)
-        first_pass(1, 0)
-        first_pass(1, 1)
-        turn_h(0, spent_end(w1_raw[1, 1]))
-        open_h(2)
-        partner_passes(2)
-        quantise_w2(0, SHARE_W2)
-        quantise_h(0, spent_end(w2_raw[0]).bitcast(BF16))
-        turn_h(1, spent_start(w2_raw[0]))
-        y_banks[0] = second_layer(0)
-        first_pass(2, 0)
-        quantise_h(1, spent_end(w1_raw[2, 0]).bitcast(BF16))
-        first_pass(2, 1)
-        stage_y(0, y_banks[0], first_two[:, :, 0:C])
+        partner_passes(0, True, False)
+        for s in range(PASSES):
+            token_pass(0, s, cast_w1(0, s, P), False, s == PASSES - 1)
+        for e in range(1, last):
+            open_h(e)
+            partner_passes(e, True, False)
+
+        quantise_w2(0, cast_w2(0, SHARE_W2), 1)
+        turn_h(0, spent_half(w2_tiles[0][:], 3))
+        first_h = keep.tile([P, HALF], F32, name="first_h", align_bytes=64)
+        quantise_h(0, first_h[:])
+        y_bank = second_layer(0)
         open_h(last)
-        first_pass(last, 0)
-        planes_of(0, spent_end(w1_raw[last, 0]).bitcast(BF16), y_staged[0])
-        turn_h(2, spent_start(w1_raw[last, 0]))
-        partner_passes(last)
-        last_pass_in_halves()
-        quantise_h(2, spent_end(w1_raw[last, 1]).bitcast(BF16))
-        quantise_w2(1, SHARE_B)
-        turn_h(last, spent_start(w2_raw[1]))
-        y_banks[1] = second_layer(1)
-        late_grouped = keep.tile([P, PACK, P * PACK], BF16, name="late", align_bytes=64)
-        h_last = fresh_bf16("h_last")
-        unturn_h(last, h_last)
-        cast_by_slices(2, late_grouped, SHARE_C)
-        quantise_last_w2(late_grouped, 2)
-        quantise_turned(last, h_last)
-        y1_rounded = spent_end(w2_raw[2]).bitcast(BF16)
-        round_y_on_scalar(y1_rounded, y_banks[1])
-        quantise_y(1, 1, y1_rounded)
-        stage_y(1, y_banks[1], first_two[:, :, C : 2 * C])
-        y_banks[2] = second_layer(2)
-        tail_grouped = keep.tile([P, PACK, P * PACK], BF16, name="tail_grouped", align_bytes=64)
-        cast_by_slices(last, tail_grouped, SHARE_A)
-        quantise_last_w2(tail_grouped)
-        y2_rounded = spent_start(w2_raw[last]).bitcast(BF16)
-        round_y_on_scalar(y2_rounded, y_banks[2])
-        quantise_y(2, 1, y2_rounded)
-        stage_y(2, y_banks[2], w2_raw[last][:, 1, :].rearrange("p (t s) -> p t s", t=PACK))
+        partner_passes(last, True, False)
+
+        pair_of_passes(1, False, True)
+        staged = [stage_y(y_bank, w1_raw[2])]
+        quantise_y(0, round_y(nc.vector.tensor_copy, staged[0], fresh_rounded(0)))
+        turn_h(1, spent_half(w1_raw[2], 3))
+
+        pair_of_passes(2, False, True)
+
+        token_pass(last, 0, cast_w1(last, 0, SHARE_W1), False, False)
+        quantise_h(1, spent_half(w1_raw[6], 3))
+
+        token_pass(last, 1, cast_w1(last, 1, SHARE_W1), False, True)
+        turn_h(2, spent_half(w1_raw[7], 3))
+
+        quantise_w2(1, cast_by_slices(1, SHARE_SLICES), 2)
+        quantise_h(2, spent_half(w2_tiles[1][:], 3))
+        turn_h(last, spent_half(w2_tiles[1][:], 2))
+        y_bank = second_layer(1)
+
+        quantise_w2(2, cast_by_slices(2, SHARE_LAST), 2)
+        quantise_h(last, spent_half(w2_tiles[2][:], 3))
+        staged.append(stage_y(y_bank, w2_tiles[2][:]))
+        y_bank = second_layer(2)
+
+        grouped = cast_by_slices(last, SHARE_LAST)
+        quantise_w2(last, grouped, 2)
         for_planes = second_layer(last)
         for_values = [second_layer(last, slices=(2 + u, u)) for u in range(2)]
-        y_last = fresh_bf16("y_last")
-        round_y(y_last, for_planes[:])
+        y_first = round_y(nc.vector.tensor_copy, staged[1], grouped[:, 0, :])
+        quantise_y(2, round_y(nc.scalar.copy, y_bank[:], spent_half(w2_tiles[last][:], 3).bitcast(BF16)))
+        quantise_y(1, y_first)
+        staged.append(stage_y(y_bank, w2_tiles[last][:]))
+        y_last = round_y(nc.vector.tensor_copy, for_planes[:], fresh_rounded(last))
         last_values = keep.tile([P, PACK, C], F32, name="last_values")
         for pair in range(2):
             nc.scalar.copy(out=last_values[:, 2 * pair : 2 * pair + 2, :], in_=for_values[pair][:, pair:PACK:2, :])
-        quantise_y(last, 1, y_last)
+        quantise_y(last, y_last)
 
-        nc.sync.dma_start(out=out0[:, :, 0 : 2 * C], in_=first_two)
-        nc.sync.dma_start(out=out1[:, 0 : 2 * C], in_=y_codes[:, 0 : 2 * C].bitcast(I32))
-        nc.sync.dma_start(out=out0[:, :, 2 * C : 3 * C], in_=y_staged[2])
+        nc.sync.dma_start(out=out1[:, 0:C], in_=y_codes[:, 0:C].bitcast(I32))
+        for e in range(last):
+            nc.sync.dma_start(out=out0[:, :, e * C : (e + 1) * C], in_=staged[e])
         nc.sync.dma_start(out=out0[:, 0:PACK:2, 3 * C : SLOTS], in_=last_values[:, 0:2, :])
         nc.scalar.dma_start(out=out0[:, 1:PACK:2, 3 * C : SLOTS], in_=last_values[:, 2:4, :])
-        nc.sync.dma_start(out=out1[:, 2 * C : SLOTS], in_=y_codes[:, 2 * C : SLOTS].bitcast(I32))
+        nc.sync.dma_start(out=out1[:, C:SLOTS], in_=y_codes[:, C:SLOTS].bitcast(I32))
         for q in range(4):
             queue = nc.sync if q < 2 else nc.scalar
             queue.dma_start(

@@ -21,10 +21,9 @@ HALF = 256
 WINDOW = 768
 FLOPS = 2 * SLOTS * (2 * K * H + H * N)
 TOKEN, PARTNER = 0, 1
-W1_LOADS = ((0, 2), (2, 4), (4, 6), (6, 7), (7, 8))
-SHARE_PAIR = 96
+W1_LOADS = ((0, 1), (1, 2), (2, 3), (3, 4), (4, 5), (5, 6), (6, 7), (7, 8))
+SHARE_EARLY = 96
 SHARE_W1 = 56
-SHARE_W2 = 56
 SHARE_SLICES = 96
 SHARE_LAST = 80
 
@@ -77,13 +76,16 @@ def tile_moe_duo_s_none_kernel(
         for r in range(4):
             nc.sync.dma_start(out=xs_dst[r:P:32], in_=xs_src[r])
         load_w1(0)
+        load_w1(1)
         wps_src = wp_scales.bitcast(I32).rearrange("e s (q r) c -> r q (e s) c", r=4)
         wps_dst = wps[:].bitcast(I32).rearrange("p (g c) -> p g c", g=E * PASSES)
         for r in range(4):
             nc.sync.dma_start(out=wps_dst[r:P:32], in_=wps_src[r])
         nc.sync.dma_start(out=wp[:].bitcast(I32), in_=wp_words.bitcast(I32).rearrange("e s p c -> p (e s) c"))
+        for n in range(2, 6):
+            load_w1(n)
         load_w2(0)
-        for n in range(1, len(W1_LOADS)):
+        for n in range(6, 8):
             load_w1(n)
         for e in range(1, E):
             load_w2(e)
@@ -131,10 +133,17 @@ def tile_moe_duo_s_none_kernel(
             shared_cast(dst, src, share)
             return grouped
 
-        def token_pass(e, s, grouped, start, stop):
+        def quantise_w1(e, s, share):
+            return quantise_cast(cast_w1(e, s, share))
+
+        def quantise_cast(grouped):
             codes = ring.tile([P, H], U32, name="w1c", align_bytes=64)
             scales = ring.tile([P, H], U8, name="w1s", align_bytes=64)
             nc.vector.quantize_mx(out=codes[:].bitcast(FP8X4), scales=scales[:], in_=grouped[:])
+            return codes, scales
+
+        def token_pass(e, s, weights, start, stop):
+            codes, scales = weights
             first_layer_pass(e, s, TOKEN, codes[:].bitcast(FP8X4), scales[:], start, stop)
 
         def turn_h(e, words):
@@ -174,22 +183,18 @@ def tile_moe_duo_s_none_kernel(
                     in_=grouped[:, t : t + step, :].rearrange("p t c -> p (t c)"),
                 )
 
-        def cast_w2(e, share):
-            grouped, dst, src = w2_views(e)
-            shared_cast(dst, src, share)
-            return grouped
-
         def cast_by_slices(e, share):
             grouped, dst, src = w2_views(e)
             nc.scalar.copy(out=dst[:, 0:share, :, 2:4], in_=src[:, 0:share, :, 2:4])
             nc.vector.tensor_copy(out=dst[:, :, :, 0:2], in_=src[:, :, :, 0:2])
-            nc.vector.tensor_copy(out=dst[:, share:P, :, 2:4], in_=src[:, share:P, :, 2:4])
+            if share < P:
+                nc.vector.tensor_copy(out=dst[:, share:P, :, 2:4], in_=src[:, share:P, :, 2:4])
             return grouped
 
         def second_layer(e, slices=range(PACK)):
             codes, scales = w2_quant[e]
             hc, hs = h_quant[e]
-            bank = psum.tile([P, PACK, C], F32, name="y_bank", bufs=4)
+            bank = psum.tile([P, PACK, C], F32, name="sums", bufs=7)
             for t in slices:
                 words = slice(t * P, (t + 1) * P)
                 nc.tensor.matmul_mx(
@@ -211,58 +216,59 @@ def tile_moe_duo_s_none_kernel(
             nc.vector.quantize_mx(out=y_codes[:, slots].bitcast(FP8X4), scales=y_scales[:, slots], in_=grouped)
 
         def open_h(e):
-            h_banks[e] = psum.tile([P, H], F32, name="h_bank", bufs=3)
-
-        def pair_of_passes(e, start, stop):
-            first = cast_w1(e, 0, 0)
-            second = cast_w1(e, 1, SHARE_PAIR)
-            token_pass(e, 0, first, start, False)
-            token_pass(e, 1, second, False, stop)
+            h_banks[e] = psum.tile([P, H], F32, name="sums", bufs=7)
 
         def spent_half(raw, row):
             return raw[:, row, HALF:]
+
+        def spent_front(raw, row):
+            return raw[:, row, 0:HALF]
 
         def stage_y(bank, raw):
             staged = raw[:, 1, :].rearrange("p (t s) -> p t s", t=PACK)
             nc.scalar.copy(out=staged, in_=bank[:])
             return staged
 
-        open_h(0)
-        partner_passes(0, True, False)
-        for s in range(PASSES):
-            token_pass(0, s, cast_w1(0, s, P), False, s == PASSES - 1)
-        for e in range(1, last):
+        for e in range(E):
             open_h(e)
             partner_passes(e, True, False)
+        for s in range(PASSES):
+            token_pass(0, s, quantise_w1(0, s, P), False, s == PASSES - 1)
+        token_pass(1, 0, quantise_w1(1, 0, SHARE_EARLY), False, False)
 
-        quantise_w2(0, cast_w2(0, SHARE_W2), 1)
-        turn_h(0, spent_half(w2_tiles[0][:], 3))
-        first_h = keep.tile([P, HALF], F32, name="first_h", align_bytes=64)
-        quantise_h(0, first_h[:])
+        weights = quantise_w1(1, 1, SHARE_W1)
+        turn_h(0, spent_half(w1_raw[3], 3))
+        token_pass(1, 1, weights, False, True)
+
+        weights = quantise_w1(2, 0, SHARE_W1)
+        quantise_h(0, spent_half(w1_raw[4], 3))
+        turn_h(1, spent_half(w1_raw[4], 2))
+        token_pass(2, 0, weights, False, False)
+
+        weights = quantise_w1(2, 1, SHARE_W1)
+        quantise_h(1, spent_half(w1_raw[5], 3))
+        token_pass(2, 1, weights, False, True)
+
+        quantise_w2(0, cast_by_slices(0, SHARE_SLICES), 2)
+        turn_h(2, spent_front(w2_tiles[0][:], 3))
         y_bank = second_layer(0)
-        open_h(last)
-        partner_passes(last, True, False)
 
-        pair_of_passes(1, False, True)
-        staged = [stage_y(y_bank, w1_raw[2])]
-        quantise_y(0, round_y(nc.vector.tensor_copy, staged[0], fresh_rounded(0)))
-        turn_h(1, spent_half(w1_raw[2], 3))
+        weights = quantise_w1(last, 0, SHARE_W1)
+        quantise_h(2, spent_half(w1_raw[6], 3))
+        staged = [stage_y(y_bank, w1_raw[6])]
+        token_pass(last, 0, weights, False, False)
 
-        pair_of_passes(2, False, True)
-
-        token_pass(last, 0, cast_w1(last, 0, SHARE_W1), False, False)
-        quantise_h(1, spent_half(w1_raw[6], 3))
-
-        token_pass(last, 1, cast_w1(last, 1, SHARE_W1), False, True)
-        turn_h(2, spent_half(w1_raw[7], 3))
+        grouped = cast_w1(last, 1, SHARE_W1)
+        y_zero = round_y(nc.vector.tensor_copy, staged[0], spent_half(w1_raw[7], 3).bitcast(BF16))
+        token_pass(last, 1, quantise_cast(grouped), False, True)
+        quantise_y(0, y_zero)
 
         quantise_w2(1, cast_by_slices(1, SHARE_SLICES), 2)
-        quantise_h(2, spent_half(w2_tiles[1][:], 3))
-        turn_h(last, spent_half(w2_tiles[1][:], 2))
+        turn_h(last, spent_front(w2_tiles[1][:], 3))
         y_bank = second_layer(1)
 
         quantise_w2(2, cast_by_slices(2, SHARE_LAST), 2)
-        quantise_h(last, spent_half(w2_tiles[2][:], 3))
+        quantise_h(last, spent_front(w2_tiles[2][:], 3))
         staged.append(stage_y(y_bank, w2_tiles[2][:]))
         y_bank = second_layer(2)
 
@@ -271,7 +277,7 @@ def tile_moe_duo_s_none_kernel(
         for_planes = second_layer(last)
         for_values = [second_layer(last, slices=(2 + u, u)) for u in range(2)]
         y_first = round_y(nc.vector.tensor_copy, staged[1], grouped[:, 0, :])
-        quantise_y(2, round_y(nc.scalar.copy, y_bank[:], spent_half(w2_tiles[last][:], 3).bitcast(BF16)))
+        quantise_y(2, round_y(nc.scalar.copy, y_bank[:], spent_front(w2_tiles[last][:], 3).bitcast(BF16)))
         quantise_y(1, y_first)
         staged.append(stage_y(y_bank, w2_tiles[last][:]))
         y_last = round_y(nc.vector.tensor_copy, for_planes[:], fresh_rounded(last))

@@ -71,16 +71,17 @@ def tile_moe_duo_s_none_kernel(
         )
         nc.sync.dma_start(out=lists[PARTNER][:], in_=offs2)
         nc.sync.dma_start(out=lists[TOKEN][:], in_=offs)
-        xs_src = x_scales.bitcast(I32).rearrange("s (q r) c -> r q s c", r=4)
-        xs_dst = xs[:, 0 : PASSES * T].bitcast(I32).rearrange("p (s c) -> p s c", s=PASSES)
-        for r in range(4):
-            nc.sync.dma_start(out=xs_dst[r:P:32], in_=xs_src[r])
-        load_w1(0)
-        load_w1(1)
         wps_src = wp_scales.bitcast(I32).rearrange("e s (q r) c -> r q (e s) c", r=4)
         wps_dst = wps[:].bitcast(I32).rearrange("p (g c) -> p g c", g=E * PASSES)
         for r in range(4):
             nc.sync.dma_start(out=wps_dst[r:P:32], in_=wps_src[r])
+        xs_src = x_scales.bitcast(I32).rearrange("s (q r) c -> r q s c", r=4)
+        xs_dst = xs[:, 0 : PASSES * T].bitcast(I32).rearrange("p (s c) -> p s c", s=PASSES)
+        nc.sync.dma_start(out=xs_dst[0:P:32], in_=xs_src[0])
+        load_w1(0)
+        for r in range(1, 4):
+            nc.sync.dma_start(out=xs_dst[r:P:32], in_=xs_src[r])
+        load_w1(1)
         nc.sync.dma_start(out=wp[:].bitcast(I32), in_=wp_words.bitcast(I32).rearrange("e s p c -> p (e s) c"))
         for n in range(2, 6):
             load_w1(n)
@@ -95,6 +96,7 @@ def tile_moe_duo_s_none_kernel(
         for a in (PARTNER, TOKEN):
             for s in range(PASSES):
                 nc.vector.tensor_copy(gw[a][s][:], xw[:, s * T : s * T + WINDOW].indirect(lists[a][:]))
+        for a in (PARTNER, TOKEN):
             for s in range(PASSES):
                 nc.vector.tensor_copy(gs[a][s][:], xs[:, s * T : s * T + WINDOW].indirect(lists[a][:]))
 

@@ -51,10 +51,11 @@ def tile_moe_duo_s_none_kernel(
         w2_tiles = [keep.tile([P, PACK, N], F32, name="w2r%d" % e, align_bytes=64) for e in range(E)]
         ident = keep.tile([P, P], F32, name="ident")
 
-        nc.gpsimd.memset(xs[:].bitcast(I32), 0)
         nc.vector.memset(wps[:].bitcast(I32), 0)
+        nc.vector.memset(xs[:].bitcast(I32), 0)
         nc.vector.memset(xw[:, PASSES * T :].bitcast(I32), 0)
-        make_identity(nc, ident[:])
+        nc.vector.memset(ident[:], 0.0)
+        make_identity(nc, ident[:], nomemset=True)
 
         w1_src = w1.rearrange("e (s p j) c -> p (e s) (j c)", s=PASSES, j=PACK)
 
@@ -70,11 +71,11 @@ def tile_moe_duo_s_none_kernel(
             in_=x_words.rearrange("s p t d -> p s (t d)").bitcast(I32),
         )
         nc.sync.dma_start(out=lists[PARTNER][:], in_=offs2)
-        nc.sync.dma_start(out=lists[TOKEN][:], in_=offs)
         wps_src = wp_scales.bitcast(I32).rearrange("e s (q r) c -> r q (e s) c", r=4)
         wps_dst = wps[:].bitcast(I32).rearrange("p (g c) -> p g c", g=E * PASSES)
         for r in range(4):
             nc.sync.dma_start(out=wps_dst[r:P:32], in_=wps_src[r])
+        nc.sync.dma_start(out=lists[TOKEN][:], in_=offs)
         xs_src = x_scales.bitcast(I32).rearrange("s (q r) c -> r q s c", r=4)
         xs_dst = xs[:, 0 : PASSES * T].bitcast(I32).rearrange("p (s c) -> p s c", s=PASSES)
         nc.sync.dma_start(out=xs_dst[0:P:32], in_=xs_src[0])

@@ -101,7 +101,7 @@ def tile_moe_duo_s_none_kernel(
             for s in range(PASSES):
                 nc.vector.tensor_copy(gs[a][s][:], xs[:, s * T : s * T + WINDOW].indirect(lists[a][:]))
 
-        y_codes = keep.tile([P, SLOTS], U32, name="y_codes", align_bytes=64)
+        first_codes = keep.tile([P, C], U32, name="first_codes", align_bytes=64)
         y_scales = keep.tile([P, SLOTS], U8, name="y_scales", align_bytes=64)
         out0 = out_0.rearrange("(p t) j -> p t j", t=PACK)
         out1 = out_1[0].rearrange("p j d -> p (j d)").bitcast(I32)
@@ -214,9 +214,8 @@ def tile_moe_duo_s_none_kernel(
             tile = keep.tile([P, C * PACK], BF16, name="y_rounded%d" % e, align_bytes=64)
             return tile[:]
 
-        def quantise_y(e, grouped):
-            slots = slice(e * C, (e + 1) * C)
-            nc.vector.quantize_mx(out=y_codes[:, slots].bitcast(FP8X4), scales=y_scales[:, slots], in_=grouped)
+        def quantise_y(e, grouped, codes):
+            nc.vector.quantize_mx(out=codes.bitcast(FP8X4), scales=y_scales[:, e * C : (e + 1) * C], in_=grouped)
 
         def open_h(e):
             h_banks[e] = psum.tile([P, H], F32, name="sums", bufs=7)
@@ -264,7 +263,7 @@ def tile_moe_duo_s_none_kernel(
         grouped = cast_w1(last, 1, SHARE_W1)
         y_zero = round_y(nc.vector.tensor_copy, staged[0], spent_half(w1_raw[7], 3).bitcast(BF16))
         token_pass(last, 1, quantise_cast(grouped), False, True)
-        quantise_y(0, y_zero)
+        quantise_y(0, y_zero, first_codes[:])
 
         quantise_w2(1, cast_by_slices(1, SHARE_SLICES), 2)
         turn_h(last, spent_front(w2_tiles[1][:], 3))
@@ -276,25 +275,26 @@ def tile_moe_duo_s_none_kernel(
         y_bank = second_layer(2)
 
         grouped = cast_by_slices(last, SHARE_LAST)
-        quantise_w2(last, grouped, 2)
+        quantise_w2(last, grouped, PACK)
         for_planes = second_layer(last)
-        for_values = [second_layer(last, slices=(2 + u, u)) for u in range(2)]
-        y_first = round_y(nc.vector.tensor_copy, staged[1], grouped[:, 0, :])
-        quantise_y(2, round_y(nc.scalar.copy, y_bank[:], spent_front(w2_tiles[last][:], 3).bitcast(BF16)))
-        quantise_y(1, y_first)
+        for_values = [second_layer(last, slices=(3 - u, 1 - u)) for u in range(2)]
+        rounded = {1: round_y(nc.vector.tensor_copy, staged[1], grouped[:, 0, :])}
         staged.append(stage_y(y_bank, w2_tiles[last][:]))
-        y_last = round_y(nc.vector.tensor_copy, for_planes[:], fresh_rounded(last))
+        rounded[2] = round_y(nc.scalar.copy, y_bank[:], spent_front(w2_tiles[last][:], 3).bitcast(BF16))
+        rounded[last] = round_y(nc.vector.tensor_copy, for_planes[:], fresh_rounded(last))
         last_values = keep.tile([P, PACK, C], F32, name="last_values")
         for pair in range(2):
-            nc.scalar.copy(out=last_values[:, 2 * pair : 2 * pair + 2, :], in_=for_values[pair][:, pair:PACK:2, :])
-        quantise_y(last, y_last)
+            nc.scalar.copy(out=last_values[:, 2 * pair : 2 * pair + 2, :], in_=for_values[pair][:, 1 - pair : PACK : 2, :])
+        late_codes = keep.tile([P, last * C], U32, name="hc%d" % last, align_bytes=64)
+        for e in range(1, E):
+            quantise_y(e, rounded[e], late_codes[:, (e - 1) * C : e * C])
 
-        nc.sync.dma_start(out=out1[:, 0:C], in_=y_codes[:, 0:C].bitcast(I32))
+        nc.sync.dma_start(out=out1[:, 0:C], in_=first_codes[:].bitcast(I32))
         for e in range(last):
             nc.sync.dma_start(out=out0[:, :, e * C : (e + 1) * C], in_=staged[e])
-        nc.sync.dma_start(out=out0[:, 0:PACK:2, 3 * C : SLOTS], in_=last_values[:, 0:2, :])
-        nc.scalar.dma_start(out=out0[:, 1:PACK:2, 3 * C : SLOTS], in_=last_values[:, 2:4, :])
-        nc.sync.dma_start(out=out1[:, C:SLOTS], in_=y_codes[:, C:SLOTS].bitcast(I32))
+        nc.sync.dma_start(out=out0[:, 1:PACK:2, 3 * C : SLOTS], in_=last_values[:, 0:2, :])
+        nc.scalar.dma_start(out=out0[:, 0:PACK:2, 3 * C : SLOTS], in_=last_values[:, 2:4, :])
+        nc.sync.dma_start(out=out1[:, C:SLOTS], in_=late_codes[:].bitcast(I32))
         for q in range(4):
             queue = nc.sync if q < 2 else nc.scalar
             queue.dma_start(

@@ -217,6 +217,14 @@ def tile_moe_duo_s_none_kernel(
         def quantise_y(e, grouped, codes):
             nc.vector.quantize_mx(out=codes.bitcast(FP8X4), scales=y_scales[:, e * C : (e + 1) * C], in_=grouped)
 
+        def warm_up(e):
+            codes, scales = w2_quant[e]
+            words = slice(N - P, N)
+            nc.tensor.matmul_mx(
+                out=h_banks[last][:], lhsT=codes[:, words].bitcast(FP8X4), lhsT_scale=scales[:, words],
+                rhs=last_weights[0][:].bitcast(FP8X4), rhs_scale=last_weights[1][:], start=True, stop=True,
+            )
+
         def open_h(e):
             h_banks[e] = psum.tile([P, H], F32, name="sums", bufs=7)
 
@@ -262,17 +270,20 @@ def tile_moe_duo_s_none_kernel(
 
         grouped = cast_w1(last, 1, SHARE_W1)
         y_zero = round_y(nc.vector.tensor_copy, staged[0], spent_half(w1_raw[7], 3).bitcast(BF16))
-        token_pass(last, 1, quantise_cast(grouped), False, True)
+        last_weights = quantise_cast(grouped)
+        token_pass(last, 1, last_weights, False, True)
         quantise_y(0, y_zero, first_codes[:])
 
         quantise_w2(1, cast_by_slices(1, SHARE_SLICES), 2)
         turn_h(last, spent_front(w2_tiles[1][:], 3))
         y_bank = second_layer(1)
+        warm_up(1)
 
         quantise_w2(2, cast_by_slices(2, SHARE_LAST), 2)
         quantise_h(last, spent_front(w2_tiles[2][:], 3))
         staged.append(stage_y(y_bank, w2_tiles[2][:]))
         y_bank = second_layer(2)
+        warm_up(2)
 
         grouped = cast_by_slices(last, SHARE_LAST)
         quantise_w2(last, grouped, PACK)

@@ -21,7 +21,7 @@ HALF = 256
 WINDOW = 768
 FLOPS = 2 * SLOTS * (2 * K * H + H * N)
 TOKEN, PARTNER = 0, 1
-W1_LOADS = ((0, 1), (1, 2), (2, 3), (3, 4), (4, 5), (5, 6), (6, 7), (7, 8))
+PIECE = PACK * H
 SHARE_EARLY = 96
 SHARE_W1 = 56
 SHARE_SLICES = 96
@@ -43,12 +43,18 @@ def tile_moe_duo_s_none_kernel(
         xs = keep.tile([P, T + WINDOW], U8, name="xs", align_bytes=64)
         wps = keep.tile([P, E * PASSES * H], U8, name="wps", align_bytes=64)
         wp = keep.tile([P, E * PASSES, 2 * H], U8, name="wp", align_bytes=64)
-        w1_tiles = [keep.tile([P, b - a, PACK * H], F32, name="w1r%d" % a, align_bytes=64) for a, b in W1_LOADS]
-        w1_raw = [
-            tile[:, g - a, :].rearrange("p (j c) -> p j c", j=PACK)
-            for tile, (a, b) in zip(w1_tiles, W1_LOADS) for g in range(a, b)
+        joined = keep.tile([P, 2 * PIECE], F32, name="joined", align_bytes=64)
+        w1_flat = [
+            joined[:, 0:PIECE] if g == 6 else keep.tile([P, PIECE], F32, name="w1r%d" % g, align_bytes=64)[:]
+            for g in range(E * PASSES)
         ]
-        w2_tiles = [keep.tile([P, PACK, N], F32, name="w2r%d" % e, align_bytes=64) for e in range(E)]
+        w2_flat = [
+            joined[:, PIECE:] if e == 2 else keep.tile([P, PIECE], F32, name="w2r%d" % e, align_bytes=64)[:]
+            for e in range(E)
+        ]
+        w1_raw = [flat.rearrange("p (j c) -> p j c", j=PACK) for flat in w1_flat]
+        w2_raw = [flat.rearrange("p (j c) -> p j c", j=PACK) for flat in w2_flat]
+        early_values = joined[:, PIECE - 7 * C : PIECE + C].rearrange("p (t s) -> p t s", t=PACK)
         ident = keep.tile([P, P], F32, name="ident")
 
         nc.vector.memset(wps[:].bitcast(I32), 0)
@@ -60,11 +66,10 @@ def tile_moe_duo_s_none_kernel(
         w1_src = w1.rearrange("e (s p j) c -> p (e s) (j c)", s=PASSES, j=PACK)
 
         def load_w1(n):
-            a, b = W1_LOADS[n]
-            nc.sync.dma_start(out=w1_tiles[n][:], in_=w1_src[:, a:b, :])
+            nc.sync.dma_start(out=w1_flat[n], in_=w1_src[:, n, :])
 
         def load_w2(e):
-            nc.sync.dma_start(out=w2_tiles[e][:], in_=w2[e].rearrange("(p j) c -> p j c", j=PACK))
+            nc.sync.dma_start(out=w2_flat[e], in_=w2[e].rearrange("(p j) c -> p (j c)", j=PACK))
 
         nc.sync.dma_start(
             out=xw[:, 0 : PASSES * T].bitcast(I32).rearrange("p (s t) -> p s t", s=PASSES),
@@ -171,7 +176,7 @@ def tile_moe_duo_s_none_kernel(
         def w2_views(e):
             grouped = ring.tile([P, PACK, P * PACK], BF16, name="grouped", bufs=4, align_bytes=64)
             dst = grouped[:].rearrange("p t (m j) -> p m j t", j=PACK)
-            src = w2_tiles[e][:].rearrange("p j (m t) -> p m j t", t=PACK)
+            src = w2_raw[e].rearrange("p j (m t) -> p m j t", t=PACK)
             return grouped, dst, src
 
         def quantise_w2(e, grouped, calls):
@@ -234,8 +239,7 @@ def tile_moe_duo_s_none_kernel(
         def spent_front(raw, row):
             return raw[:, row, 0:HALF]
 
-        def stage_y(bank, raw):
-            staged = raw[:, 1, :].rearrange("p (t s) -> p t s", t=PACK)
+        def stage_y(bank, staged):
             nc.scalar.copy(out=staged, in_=bank[:])
             return staged
 
@@ -260,12 +264,12 @@ def tile_moe_duo_s_none_kernel(
         token_pass(2, 1, weights, False, True)
 
         quantise_w2(0, cast_by_slices(0, SHARE_SLICES), 2)
-        turn_h(2, spent_front(w2_tiles[0][:], 3))
+        turn_h(2, spent_front(w2_raw[0], 3))
         y_bank = second_layer(0)
 
         weights = quantise_w1(last, 0, SHARE_W1)
-        quantise_h(2, spent_half(w1_raw[6], 3))
-        staged = [stage_y(y_bank, w1_raw[6])]
+        quantise_h(2, spent_half(w1_raw[6], 1))
+        staged = [stage_y(y_bank, early_values[:, :, 0:C])]
         token_pass(last, 0, weights, False, False)
 
         grouped = cast_w1(last, 1, SHARE_W1)
@@ -275,13 +279,13 @@ def tile_moe_duo_s_none_kernel(
         quantise_y(0, y_zero, first_codes[:])
 
         quantise_w2(1, cast_by_slices(1, SHARE_SLICES), 2)
-        turn_h(last, spent_front(w2_tiles[1][:], 3))
+        turn_h(last, spent_front(w2_raw[1], 3))
         y_bank = second_layer(1)
         warm_up(1)
 
         quantise_w2(2, cast_by_slices(2, SHARE_LAST), 2)
-        quantise_h(last, spent_front(w2_tiles[2][:], 3))
-        staged.append(stage_y(y_bank, w2_tiles[2][:]))
+        quantise_h(last, spent_front(w2_raw[2], 3))
+        staged.append(stage_y(y_bank, early_values[:, :, C : 2 * C]))
         y_bank = second_layer(2)
         warm_up(2)
 
@@ -290,8 +294,8 @@ def tile_moe_duo_s_none_kernel(
         for_planes = second_layer(last)
         for_values = [second_layer(last, slices=(3 - u, 1 - u)) for u in range(2)]
         rounded = {1: round_y(nc.vector.tensor_copy, staged[1], grouped[:, 0, :])}
-        staged.append(stage_y(y_bank, w2_tiles[last][:]))
-        rounded[2] = round_y(nc.scalar.copy, y_bank[:], spent_front(w2_tiles[last][:], 3).bitcast(BF16))
+        staged.append(stage_y(y_bank, w2_raw[last][:, 1, :].rearrange("p (t s) -> p t s", t=PACK)))
+        rounded[2] = round_y(nc.scalar.copy, y_bank[:], spent_front(w2_raw[last], 3).bitcast(BF16))
         rounded[last] = round_y(nc.vector.tensor_copy, for_planes[:], fresh_rounded(last))
         last_values = keep.tile([P, PACK, C], F32, name="last_values")
         for pair in range(2):
@@ -301,8 +305,8 @@ def tile_moe_duo_s_none_kernel(
             quantise_y(e, rounded[e], late_codes[:, (e - 1) * C : e * C])
 
         nc.sync.dma_start(out=out1[:, 0:C], in_=first_codes[:].bitcast(I32))
-        for e in range(last):
-            nc.sync.dma_start(out=out0[:, :, e * C : (e + 1) * C], in_=staged[e])
+        nc.sync.dma_start(out=out0[:, :, 0 : 2 * C], in_=early_values)
+        nc.sync.dma_start(out=out0[:, :, 2 * C : 3 * C], in_=staged[2])
         nc.sync.dma_start(out=out0[:, 1:PACK:2, 3 * C : SLOTS], in_=last_values[:, 0:2, :])
         nc.scalar.dma_start(out=out0[:, 0:PACK:2, 3 * C : SLOTS], in_=last_values[:, 2:4, :])
         nc.sync.dma_start(out=out1[:, C:SLOTS], in_=late_codes[:].bitcast(I32))

@@ -38,18 +38,18 @@ def tile_moe_duo_s_none_kernel(
         ring = ctx.enter_context(tc.tile_pool(name="ring", bufs=3))
         psum = ctx.enter_context(tc.psum_pool(name="psum", bufs=2))
 
-        lists = [keep.tile([P, SLOTS // 16], U16, name="list%d" % a) for a in range(2)]
-        xw = keep.tile([P, T + WINDOW], U32, name="xw", align_bytes=64)
-        xs = keep.tile([P, T + WINDOW], U8, name="xs", align_bytes=64)
-        wps = keep.tile([P, E * PASSES * H], U8, name="wps", align_bytes=64)
-        wp = keep.tile([P, E * PASSES, 2 * H], U8, name="wp", align_bytes=64)
-        joined = keep.tile([P, 2 * PIECE], F32, name="joined", align_bytes=64)
+        lists = [keep.tile([P, SLOTS // 16], U16, name="list%d" % a, align_bytes=256) for a in range(2)]
+        xw = keep.tile([P, T + WINDOW], U32, name="xw", align_bytes=256)
+        xs = keep.tile([P, T + WINDOW], U8, name="xs", align_bytes=256)
+        wps = keep.tile([P, E * PASSES * H], U8, name="wps", align_bytes=256)
+        wp = keep.tile([P, E * PASSES, 2 * H], U8, name="wp", align_bytes=256)
+        joined = keep.tile([P, 2 * PIECE], F32, name="joined", align_bytes=256)
         w1_flat = [
-            joined[:, 0:PIECE] if g == 6 else keep.tile([P, PIECE], F32, name="w1r%d" % g, align_bytes=64)[:]
+            joined[:, 0:PIECE] if g == 6 else keep.tile([P, PIECE], F32, name="w1r%d" % g, align_bytes=256)[:]
             for g in range(E * PASSES)
         ]
         w2_flat = [
-            joined[:, PIECE:] if e == 2 else keep.tile([P, PIECE], F32, name="w2r%d" % e, align_bytes=64)[:]
+            joined[:, PIECE:] if e == 2 else keep.tile([P, PIECE], F32, name="w2r%d" % e, align_bytes=256)[:]
             for e in range(E)
         ]
         w1_raw = [flat.rearrange("p (j c) -> p j c", j=PACK) for flat in w1_flat]
@@ -97,8 +97,8 @@ def tile_moe_duo_s_none_kernel(
         for e in range(1, E):
             load_w2(e)
 
-        gw = [[keep.tile([P, SLOTS], U32, name="gw%d_%d" % (a, s), align_bytes=64) for s in range(PASSES)] for a in range(2)]
-        gs = [[keep.tile([P, SLOTS], U8, name="gs%d_%d" % (a, s), align_bytes=64) for s in range(PASSES)] for a in range(2)]
+        gw = [[keep.tile([P, SLOTS], U32, name="gw%d_%d" % (a, s), align_bytes=256) for s in range(PASSES)] for a in range(2)]
+        gs = [[keep.tile([P, SLOTS], U8, name="gs%d_%d" % (a, s), align_bytes=256) for s in range(PASSES)] for a in range(2)]
         for a in (PARTNER, TOKEN):
             for s in range(PASSES):
                 nc.vector.tensor_copy(gw[a][s][:], xw[:, s * T : s * T + WINDOW].indirect(lists[a][:]))
@@ -106,8 +106,8 @@ def tile_moe_duo_s_none_kernel(
             for s in range(PASSES):
                 nc.vector.tensor_copy(gs[a][s][:], xs[:, s * T : s * T + WINDOW].indirect(lists[a][:]))
 
-        first_codes = keep.tile([P, C], U32, name="first_codes", align_bytes=64)
-        y_scales = keep.tile([P, SLOTS], U8, name="y_scales", align_bytes=64)
+        first_codes = keep.tile([P, C], U32, name="first_codes", align_bytes=256)
+        y_scales = keep.tile([P, SLOTS], U8, name="y_scales", align_bytes=256)
         out0 = out_0.rearrange("(p t) j -> p t j", t=PACK)
         out1 = out_1[0].rearrange("p j d -> p (j d)").bitcast(I32)
 
@@ -168,8 +168,8 @@ def tile_moe_duo_s_none_kernel(
                 out=words.rearrange("p (s u) -> p s u", u=2),
                 in_=turned[e][:].rearrange("p u s -> p s u"),
             )
-            codes = keep.tile([P, C], U32, name="hc%d" % e, align_bytes=64)
-            scales = keep.tile([P, C], U8, name="hs%d" % e, align_bytes=64)
+            codes = keep.tile([P, C], U32, name="hc%d" % e, align_bytes=256)
+            scales = keep.tile([P, C], U8, name="hs%d" % e, align_bytes=256)
             nc.vector.quantize_mx(out=codes[:].bitcast(FP8X4), scales=scales[:], in_=words.bitcast(BF16))
             h_quant[e] = (codes, scales)
 
@@ -215,8 +215,15 @@ def tile_moe_duo_s_none_kernel(
             copy(out=grouped.rearrange("p (s t) -> p s t", t=PACK), in_=values.rearrange("p t s -> p s t"))
             return grouped
 
+        def round_staged(values, grouped):
+            nc.vector.tensor_copy(
+                out=grouped.rearrange("p (c i t) -> p c t i", i=4, t=PACK),
+                in_=values.rearrange("p t (c i) -> p c t i", i=4),
+            )
+            return grouped
+
         def fresh_rounded(e):
-            tile = keep.tile([P, C * PACK], BF16, name="y_rounded%d" % e, align_bytes=64)
+            tile = keep.tile([P, C * PACK], BF16, name="y_rounded%d" % e, align_bytes=256)
             return tile[:]
 
         def quantise_y(e, grouped, codes):
@@ -273,7 +280,7 @@ def tile_moe_duo_s_none_kernel(
         token_pass(last, 0, weights, False, False)
 
         grouped = cast_w1(last, 1, SHARE_W1)
-        y_zero = round_y(nc.vector.tensor_copy, staged[0], spent_half(w1_raw[7], 3).bitcast(BF16))
+        y_zero = round_staged(staged[0], spent_half(w1_raw[7], 3).bitcast(BF16))
         last_weights = quantise_cast(grouped)
         token_pass(last, 1, last_weights, False, True)
         quantise_y(0, y_zero, first_codes[:])
@@ -293,14 +300,14 @@ def tile_moe_duo_s_none_kernel(
         quantise_w2(last, grouped, PACK)
         for_planes = second_layer(last)
         for_values = [second_layer(last, slices=(3 - u, 1 - u)) for u in range(2)]
-        rounded = {1: round_y(nc.vector.tensor_copy, staged[1], grouped[:, 0, :])}
+        rounded = {1: round_staged(staged[1], grouped[:, 0, :])}
         staged.append(stage_y(y_bank, w2_raw[last][:, 1, :].rearrange("p (t s) -> p t s", t=PACK)))
         rounded[2] = round_y(nc.scalar.copy, y_bank[:], spent_front(w2_raw[last], 3).bitcast(BF16))
         rounded[last] = round_y(nc.vector.tensor_copy, for_planes[:], fresh_rounded(last))
-        last_values = keep.tile([P, PACK, C], F32, name="last_values")
+        last_values = keep.tile([P, PACK, C], F32, name="last_values", align_bytes=256)
         for pair in range(2):
             nc.scalar.copy(out=last_values[:, 2 * pair : 2 * pair + 2, :], in_=for_values[pair][:, 1 - pair : PACK : 2, :])
-        late_codes = keep.tile([P, last * C], U32, name="hc%d" % last, align_bytes=64)
+        late_codes = keep.tile([P, last * C], U32, name="hc%d" % last, align_bytes=256)
         for e in range(1, E):
             quantise_y(e, rounded[e], late_codes[:, (e - 1) * C : e * C])
 

@@ -19,6 +19,7 @@ PASSES = K // (P * PACK)
 SLOTS = E * C
 HALF = 256
 WINDOW = 768
+FIRST_TOKENS = 384
 FLOPS = 2 * SLOTS * (2 * K * H + H * N)
 TOKEN, PARTNER = 0, 1
 PIECE = PACK * H
@@ -71,10 +72,10 @@ def tile_moe_duo_s_none_kernel(
         def load_w2(e):
             nc.sync.dma_start(out=w2_flat[e], in_=w2[e].rearrange("(p j) c -> p (j c)", j=PACK))
 
-        nc.sync.dma_start(
-            out=xw[:, 0 : PASSES * T].bitcast(I32).rearrange("p (s t) -> p s t", s=PASSES),
-            in_=x_words.rearrange("s p t d -> p s (t d)").bitcast(I32),
-        )
+        xw_dst = xw[:, 0 : PASSES * T].bitcast(I32).rearrange("p (s t) -> p s t", s=PASSES)
+        xw_src = x_words.rearrange("s p t d -> p s (t d)").bitcast(I32)
+        for tokens in (slice(0, FIRST_TOKENS), slice(FIRST_TOKENS, T)):
+            nc.sync.dma_start(out=xw_dst[:, :, tokens], in_=xw_src[:, :, tokens])
         nc.sync.dma_start(out=lists[PARTNER][:], in_=offs2)
         wps_src = wp_scales.bitcast(I32).rearrange("e s (q r) c -> r q (e s) c", r=4)
         wps_dst = wps[:].bitcast(I32).rearrange("p (g c) -> p g c", g=E * PASSES)
@@ -83,9 +84,8 @@ def tile_moe_duo_s_none_kernel(
         nc.sync.dma_start(out=lists[TOKEN][:], in_=offs)
         xs_src = x_scales.bitcast(I32).rearrange("s (q r) c -> r q s c", r=4)
         xs_dst = xs[:, 0 : PASSES * T].bitcast(I32).rearrange("p (s c) -> p s c", s=PASSES)
-        nc.sync.dma_start(out=xs_dst[0:P:32], in_=xs_src[0])
         load_w1(0)
-        for r in range(1, 4):
+        for r in range(4):
             nc.sync.dma_start(out=xs_dst[r:P:32], in_=xs_src[r])
         load_w1(1)
         nc.sync.dma_start(out=wp[:].bitcast(I32), in_=wp_words.bitcast(I32).rearrange("e s p c -> p (e s) c"))

from contextlib import ExitStack

import concourse.mybir as mybir
from concourse.masks import make_identity

F32 = mybir.dt.float32
BF16 = mybir.dt.bfloat16
I32 = mybir.dt.int32
U32 = mybir.dt.uint32
U16 = mybir.dt.uint16
U8 = mybir.dt.uint8
FP8X4 = mybir.dt.float8_e4m3fn_x4
FP4X4 = mybir.dt.float4_e2m1fn_x4

K, T, E, C, H, N = 1024, 512, 4, 128, 512, 512
P = 128
PACK = 4
PASSES = K // (P * PACK)
SLOTS = E * C
HALF = 256
WINDOW = 768
FIRST_TOKENS = 384
FLOPS = 2 * SLOTS * (2 * K * H + H * N)
TOKEN, PARTNER = 0, 1
PIECE = PACK * H
SHARE_EARLY = 96
SHARE_W1 = 56
SHARE_SLICES = 96
SHARE_LAST = 80


def tile_moe_duo_s_none_kernel(
    tc, x_words, x_scales, w1, wp_words, wp_scales, w2, offs, offs2, out_0, out_1, out_2
):
    nc = tc.nc
    last = E - 1
    with ExitStack() as ctx:
        keep = ctx.enter_context(tc.tile_pool(name="keep", bufs=1))
        ring = ctx.enter_context(tc.tile_pool(name="ring", bufs=3))
        psum = ctx.enter_context(tc.psum_pool(name="psum", bufs=2))

        lists = [keep.tile([P, SLOTS // 16], U16, name="list%d" % a, align_bytes=256) for a in range(2)]
        xw = keep.tile([P, T + WINDOW], U32, name="xw", align_bytes=256)
        xs = keep.tile([P, T + WINDOW], U8, name="xs", align_bytes=256)
        wps = keep.tile([P, E * PASSES * H], U8, name="wps", align_bytes=256)
        wp = keep.tile([P, E * PASSES, 2 * H], U8, name="wp", align_bytes=256)
        joined = keep.tile([P, 2 * PIECE], F32, name="joined", align_bytes=256)
        w1_flat = [
            joined[:, 0:PIECE] if g == 6 else keep.tile([P, PIECE], F32, name="w1r%d" % g, align_bytes=256)[:]
            for g in range(E * PASSES)
        ]
        w2_flat = [
            joined[:, PIECE:] if e == 2 else keep.tile([P, PIECE], F32, name="w2r%d" % e, align_bytes=256)[:]
            for e in range(E)
        ]
        w1_raw = [flat.rearrange("p (j c) -> p j c", j=PACK) for flat in w1_flat]
        w2_raw = [flat.rearrange("p (j c) -> p j c", j=PACK) for flat in w2_flat]
        early_values = joined[:, PIECE - 7 * C : PIECE + C].rearrange("p (t s) -> p t s", t=PACK)
        ident = keep.tile([P, P], F32, name="ident")

        nc.vector.memset(wps[:].bitcast(I32), 0)
        nc.vector.memset(xs[:].bitcast(I32), 0)
        nc.vector.memset(xw[:, PASSES * T :].bitcast(I32), 0)
        nc.vector.memset(ident[:], 0.0)
        make_identity(nc, ident[:], nomemset=True)

        w1_src = w1.rearrange("e (s p j) c -> p (e s) (j c)", s=PASSES, j=PACK)

        def load_w1(n):
            nc.sync.dma_start(out=w1_flat[n], in_=w1_src[:, n, :])

        def load_w2(e):
            nc.sync.dma_start(out=w2_flat[e], in_=w2[e].rearrange("(p j) c -> p (j c)", j=PACK))

        xw_dst = xw[:, 0 : PASSES * T].bitcast(I32).rearrange("p (s t) -> p s t", s=PASSES)
        xw_src = x_words.rearrange("s p t d -> p s (t d)").bitcast(I32)
        for tokens in (slice(0, FIRST_TOKENS), slice(FIRST_TOKENS, T)):
            nc.sync.dma_start(out=xw_dst[:, :, tokens], in_=xw_src[:, :, tokens])
        nc.sync.dma_start(out=lists[PARTNER][:], in_=offs2)
        wps_src = wp_scales.bitcast(I32).rearrange("e s (q r) c -> r q (e s) c", r=4)
        wps_dst = wps[:].bitcast(I32).rearrange("p (g c) -> p g c", g=E * PASSES)
        for r in range(4):
            nc.sync.dma_start(out=wps_dst[r:P:32], in_=wps_src[r])
        nc.sync.dma_start(out=lists[TOKEN][:], in_=offs)
        xs_src = x_scales.bitcast(I32).rearrange("s (q r) c -> r q s c", r=4)
        xs_dst = xs[:, 0 : PASSES * T].bitcast(I32).rearrange("p (s c) -> p s c", s=PASSES)
        load_w1(0)
        for r in range(4):
            nc.sync.dma_start(out=xs_dst[r:P:32], in_=xs_src[r])
        load_w1(1)
        nc.sync.dma_start(out=wp[:].bitcast(I32), in_=wp_words.bitcast(I32).rearrange("e s p c -> p (e s) c"))
        for n in range(2, 6):
            load_w1(n)
        load_w2(0)
        for n in range(6, 8):
            load_w1(n)
        for e in range(1, E):
            load_w2(e)

        gw = [[keep.tile([P, SLOTS], U32, name="gw%d_%d" % (a, s), align_bytes=256) for s in range(PASSES)] for a in range(2)]
        gs = [[keep.tile([P, SLOTS], U8, name="gs%d_%d" % (a, s), align_bytes=256) for s in range(PASSES)] for a in range(2)]
        for a in (PARTNER, TOKEN):
            for s in range(PASSES):
                nc.vector.tensor_copy(gw[a][s][:], xw[:, s * T : s * T + WINDOW].indirect(lists[a][:]))
        for a in (PARTNER, TOKEN):
            for s in range(PASSES):
                nc.vector.tensor_copy(gs[a][s][:], xs[:, s * T : s * T + WINDOW].indirect(lists[a][:]))

        first_codes = keep.tile([P, C], U32, name="first_codes", align_bytes=256)
        y_scales = keep.tile([P, SLOTS], U8, name="y_scales", align_bytes=256)
        out0 = out_0.rearrange("(p t) j -> p t j", t=PACK)
        out1 = out_1[0].rearrange("p j d -> p (j d)").bitcast(I32)

        h_banks, turned, h_quant, w2_quant = {}, {}, {}, {}

        def first_layer_pass(e, s, side, rhs, rhs_scale, start, stop):
            slots = slice(e * C, (e + 1) * C)
            nc.tensor.matmul_mx(
                out=h_banks[e][:], lhsT=gw[side][s][:, slots].bitcast(FP8X4), lhsT_scale=gs[side][s][:, slots],
                rhs=rhs, rhs_scale=rhs_scale, start=start, stop=stop,
            )

        def partner_passes(e, start, stop):
            for s in range(PASSES):
                g = e * PASSES + s
                first_layer_pass(
                    e, s, PARTNER, wp[:, g, :].bitcast(FP4X4), wps[:, g * H : (g + 1) * H],
                    start and s == 0, stop and s == PASSES - 1,
                )

        def shared_cast(dst, src, share):
            if share:
                nc.scalar.copy(out=dst[:, 0:share], in_=src[:, 0:share])
            if share < P:
                nc.vector.tensor_copy(out=dst[:, share:P], in_=src[:, share:P])

        def cast_w1(e, s, share):
            grouped = ring.tile([P, H * PACK], BF16, name="grouped", bufs=4, align_bytes=64)
            dst = grouped[:].rearrange("p (c i j) -> p c j i", i=4, j=PACK)
            src = w1_raw[e * PASSES + s].rearrange("p j (c i) -> p c j i", i=4)
            shared_cast(dst, src, share)
            return grouped

        def quantise_w1(e, s, share):
            return quantise_cast(cast_w1(e, s, share))

        def quantise_cast(grouped):
            codes = ring.tile([P, H], U32, name="w1c", align_bytes=64)
            scales = ring.tile([P, H], U8, name="w1s", align_bytes=64)
            nc.vector.quantize_mx(out=codes[:].bitcast(FP8X4), scales=scales[:], in_=grouped[:])
            return codes, scales

        def token_pass(e, s, weights, start, stop):
            codes, scales = weights
            first_layer_pass(e, s, TOKEN, codes[:].bitcast(FP8X4), scales[:], start, stop)

        def turn_h(e, words):
            pairs = words.rearrange("s (u p) -> s u p", u=2)
            dst = pairs.bitcast(BF16).rearrange("s u (p d) -> s u p d", d=2)
            nc.scalar.copy(out=dst, in_=h_banks[e][:].rearrange("s (p u d) -> s u p d", u=2, d=2))
            bank = psum.tile([P, 2, C], F32, name="turned", bufs=1)
            turned[e] = bank
            for u in range(2):
                nc.tensor.transpose(bank[:, u, :], pairs[:, u, :], ident[:])

        def quantise_h(e, words):
            nc.scalar.copy(
                out=words.rearrange("p (s u) -> p s u", u=2),
                in_=turned[e][:].rearrange("p u s -> p s u"),
            )
            codes = keep.tile([P, C], U32, name="hc%d" % e, align_bytes=256)
            scales = keep.tile([P, C], U8, name="hs%d" % e, align_bytes=256)
            nc.vector.quantize_mx(out=codes[:].bitcast(FP8X4), scales=scales[:], in_=words.bitcast(BF16))
            h_quant[e] = (codes, scales)

        def w2_views(e):
            grouped = ring.tile([P, PACK, P * PACK], BF16, name="grouped", bufs=4, align_bytes=64)
            dst = grouped[:].rearrange("p t (m j) -> p m j t", j=PACK)
            src = w2_raw[e].rearrange("p j (m t) -> p m j t", t=PACK)
            return grouped, dst, src

        def quantise_w2(e, grouped, calls):
            codes = ring.tile([P, N], U32, name="w2c", align_bytes=64)
            scales = ring.tile([P, N], U8, name="w2s", align_bytes=64)
            w2_quant[e] = (codes, scales)
            step = PACK // calls
            for t in range(0, PACK, step):
                words = slice(t * P, (t + step) * P)
                nc.vector.quantize_mx(
                    out=codes[:, words].bitcast(FP8X4), scales=scales[:, words],
                    in_=grouped[:, t : t + step, :].rearrange("p t c -> p (t c)"),
                )

        def cast_by_slices(e, share):
            grouped, dst, src = w2_views(e)
            nc.scalar.copy(out=dst[:, 0:share, :, 2:4], in_=src[:, 0:share, :, 2:4])
            nc.vector.tensor_copy(out=dst[:, :, :, 0:2], in_=src[:, :, :, 0:2])
            if share < P:
                nc.vector.tensor_copy(out=dst[:, share:P, :, 2:4], in_=src[:, share:P, :, 2:4])
            return grouped

        def second_layer(e, slices=range(PACK)):
            codes, scales = w2_quant[e]
            hc, hs = h_quant[e]
            bank = psum.tile([P, PACK, C], F32, name="sums", bufs=7)
            for t in slices:
                words = slice(t * P, (t + 1) * P)
                nc.tensor.matmul_mx(
                    out=bank[:, t, :], lhsT=codes[:, words].bitcast(FP8X4), lhsT_scale=scales[:, words],
                    rhs=hc[:].bitcast(FP8X4), rhs_scale=hs[:], start=True, stop=True,
                )
            return bank

        def round_y(copy, values, grouped):
            copy(out=grouped.rearrange("p (s t) -> p s t", t=PACK), in_=values.rearrange("p t s -> p s t"))
            return grouped

        def round_staged(values, grouped):
            nc.vector.tensor_copy(
                out=grouped.rearrange("p (c i t) -> p c t i", i=4, t=PACK),
                in_=values.rearrange("p t (c i) -> p c t i", i=4),
            )
            return grouped

        def fresh_rounded(e):
            tile = keep.tile([P, C * PACK], BF16, name="y_rounded%d" % e, align_bytes=256)
            return tile[:]

        def quantise_y(e, grouped, codes):
            nc.vector.quantize_mx(out=codes.bitcast(FP8X4), scales=y_scales[:, e * C : (e + 1) * C], in_=grouped)

        def warm_up(e):
            codes, scales = w2_quant[e]
            words = slice(N - P, N)
            nc.tensor.matmul_mx(
                out=h_banks[last][:], lhsT=codes[:, words].bitcast(FP8X4), lhsT_scale=scales[:, words],
                rhs=last_weights[0][:].bitcast(FP8X4), rhs_scale=last_weights[1][:], start=True, stop=True,
            )

        def open_h(e):
            h_banks[e] = psum.tile([P, H], F32, name="sums", bufs=7)

        def spent_half(raw, row):
            return raw[:, row, HALF:]

        def spent_front(raw, row):
            return raw[:, row, 0:HALF]

        def stage_y(bank, staged):
            nc.scalar.copy(out=staged, in_=bank[:])
            return staged

        for e in range(E):
            open_h(e)
            partner_passes(e, True, False)
        for s in range(PASSES):
            token_pass(0, s, quantise_w1(0, s, P), False, s == PASSES - 1)
        token_pass(1, 0, quantise_w1(1, 0, SHARE_EARLY), False, False)

        weights = quantise_w1(1, 1, SHARE_W1)
        turn_h(0, spent_half(w1_raw[3], 3))
        token_pass(1, 1, weights, False, True)

        weights = quantise_w1(2, 0, SHARE_W1)
        quantise_h(0, spent_half(w1_raw[4], 3))
        turn_h(1, spent_half(w1_raw[4], 2))
        token_pass(2, 0, weights, False, False)

        weights = quantise_w1(2, 1, SHARE_W1)
        quantise_h(1, spent_half(w1_raw[5], 3))
        token_pass(2, 1, weights, False, True)

        quantise_w2(0, cast_by_slices(0, SHARE_SLICES), 2)
        turn_h(2, spent_front(w2_raw[0], 3))
        y_bank = second_layer(0)

        weights = quantise_w1(last, 0, SHARE_W1)
        quantise_h(2, spent_half(w1_raw[6], 1))
        staged = [stage_y(y_bank, early_values[:, :, 0:C])]
        token_pass(last, 0, weights, False, False)

        grouped = cast_w1(last, 1, SHARE_W1)
        y_zero = round_staged(staged[0], spent_half(w1_raw[7], 3).bitcast(BF16))
        last_weights = quantise_cast(grouped)
        token_pass(last, 1, last_weights, False, True)
        quantise_y(0, y_zero, first_codes[:])

        quantise_w2(1, cast_by_slices(1, SHARE_SLICES), 2)
        turn_h(last, spent_front(w2_raw[1], 3))
        y_bank = second_layer(1)
        warm_up(1)

        quantise_w2(2, cast_by_slices(2, SHARE_LAST), 2)
        quantise_h(last, spent_front(w2_raw[2], 3))
        staged.append(stage_y(y_bank, early_values[:, :, C : 2 * C]))
        y_bank = second_layer(2)
        warm_up(2)

        grouped = cast_by_slices(last, SHARE_LAST)
        quantise_w2(last, grouped, PACK)
        for_planes = second_layer(last)
        for_values = [second_layer(last, slices=(3 - u, 1 - u)) for u in range(2)]
        rounded = {1: round_staged(staged[1], grouped[:, 0, :])}
        staged.append(stage_y(y_bank, w2_raw[last][:, 1, :].rearrange("p (t s) -> p t s", t=PACK)))
        rounded[2] = round_y(nc.scalar.copy, y_bank[:], spent_front(w2_raw[last], 3).bitcast(BF16))
        rounded[last] = round_y(nc.vector.tensor_copy, for_planes[:], fresh_rounded(last))
        last_values = keep.tile([P, PACK, C], F32, name="last_values", align_bytes=256)
        for pair in range(2):
            nc.scalar.copy(out=last_values[:, 2 * pair : 2 * pair + 2, :], in_=for_values[pair][:, 1 - pair : PACK : 2, :])
        late_codes = keep.tile([P, last * C], U32, name="hc%d" % last, align_bytes=256)
        for e in range(1, E):
            quantise_y(e, rounded[e], late_codes[:, (e - 1) * C : e * C])

        nc.sync.dma_start(out=out1[:, 0:C], in_=first_codes[:].bitcast(I32))
        nc.sync.dma_start(out=out0[:, :, 0 : 2 * C], in_=early_values)
        nc.sync.dma_start(out=out0[:, :, 2 * C : 3 * C], in_=staged[2])
        nc.sync.dma_start(out=out0[:, 1:PACK:2, 3 * C : SLOTS], in_=last_values[:, 0:2, :])
        nc.scalar.dma_start(out=out0[:, 0:PACK:2, 3 * C : SLOTS], in_=last_values[:, 2:4, :])
        nc.sync.dma_start(out=out1[:, C:SLOTS], in_=late_codes[:].bitcast(I32))
        for q in range(4):
            queue = nc.sync if q < 2 else nc.scalar
            queue.dma_start(
                out=out_2[0, 4 * q : 4 * q + 4, :].bitcast(I32),
                in_=y_scales[32 * q : 32 * q + 4, :].bitcast(I32),
            )
